import numpy as np
import ml_dtypes


def mxq(x, axis, fmt="e4m3"):
    dtype, down = {"e4m3": (ml_dtypes.float8_e4m3fn, 7), "e5m2": (ml_dtypes.float8_e5m2, 14)}[fmt]
    v = np.moveaxis(np.asarray(x, np.float32).astype(ml_dtypes.bfloat16).astype(np.float64), axis, -1)
    blocks = v.reshape(v.shape[:-1] + (-1, 32))
    amax = np.abs(blocks).max(-1, keepdims=True)
    byte = np.maximum(np.where(amax > 0, np.frexp(amax)[1] - 1 + 127, 0) - down, 1)
    scale = np.exp2(byte - 127.0)
    codes = (blocks / scale).astype(np.float32).astype(dtype).astype(np.float64)
    return np.moveaxis((codes * scale).reshape(v.shape), -1, axis)


WIDE = False


def mx_kscale(k):
    if not WIDE:
        return np.ones(k)
    levels = np.array([10, -10, 5, -5, 0])
    if k % 512:
        return np.exp2(np.random.permutation(np.resize(levels, k // 32))).repeat(32)
    a = np.empty((k // 512, 16))
    for p in range(k // 512):
        a[p, :8] = np.random.permutation(np.resize(levels, 8))
        for g in range(8):
            far = levels[np.abs(levels - a[p, g]) >= 10]
            a[p, g + 8] = far[np.random.randint(len(far))]
    return np.exp2(a.ravel()).repeat(32)


def f64(x):
    return np.asarray(x).astype(np.float64)


def striped(idx):
    return np.tile(idx.reshape(-1, 16).T, (8, 1)).astype(np.uint16)


def unstriped(offs):
    return offs[:16].T.reshape(-1).astype(np.int64)


E2M1 = np.array([0.0, 0.5, 1.0, 1.5, 2.0, 3.0, 4.0, 6.0, -0.0, -0.5, -1.0, -1.5, -2.0, -3.0, -4.0, -6.0])


def pack_weight(w, fmt):
    k, n = w.shape
    w = f64(np.asarray(w, np.float32).astype(ml_dtypes.bfloat16)).reshape(k // 32, 32, n)
    amax = np.abs(w).max(1)
    if fmt == "e4m3":
        byte = np.frexp(amax)[1] - 1 + 127 - 7
    else:
        mant, ex = np.frexp(amax / 6.0)
        byte = np.where(mant > 0.5, ex, ex - 1) + 127
    byte = np.clip(np.where(amax > 0, byte, 1), 1, 254)
    scaled = (w * np.exp2(127.0 - byte)[:, None, :]).reshape(k, n).astype(np.float32)
    by_word = np.ascontiguousarray(scaled.reshape(k // 512, 128, 4, n).transpose(0, 1, 3, 2))
    if fmt == "e4m3":
        words = by_word.astype(ml_dtypes.float8_e4m3fn).view(np.uint8)
    else:
        c = by_word.astype(ml_dtypes.float4_e2m1fn).view(np.uint8) & 0xF
        words = (c[..., 0::2] | (c[..., 1::2] << 4)).reshape(k // 512, 128, 2 * n)
    return np.ascontiguousarray(words), np.ascontiguousarray(byte.astype(np.uint8).reshape(k // 512, 16, n))


def unpack_weight(words, scales, fmt):
    g, _, n = scales.shape
    words = np.ascontiguousarray(words).reshape(g, 128, n, -1)
    if fmt == "e4m3":
        vals = words.view(ml_dtypes.float8_e4m3fn).astype(np.float64)
    else:
        nib = np.empty((g, 128, n, 4), np.uint8)
        nib[..., 0::2] = words & 0xF
        nib[..., 1::2] = words >> 4
        vals = E2M1[nib]
    vals = vals * np.repeat(np.exp2(scales.astype(np.float64) - 127.0), 8, axis=1)[..., None]
    return vals.transpose(0, 1, 3, 2).reshape(g * 512, n)


def gelu(v):
    return 0.5 * v * (1.0 + np.tanh(np.sqrt(2.0 / np.pi) * (v + 0.044715 * v**3)))


K, T, T2, S, P, H, N = 1024, 2048, 2048, 1024, 1024, 512, 256

def setup_inputs():
    n = np.random.standard_normal
    s = mx_kscale(K)[:, None]
    u = mx_kscale(H)[:, None]
    tab_words, tab_scales = pack_weight(n((K, T)) * s, "e4m3")
    w4_words, w4_scales = pack_weight(1.5 * n((H, N)) / np.sqrt(H) / u, "e2m1")
    return {
        "tab_words": tab_words, "tab_scales": tab_scales,
        "offs": striped(np.random.permutation(T)[:P]),
        "offs2": striped(np.random.permutation(T2)[:S]),
        "offs3": striped(np.random.permutation(T2)[:P]),
        "xs": (np.round(16 * n((K, S))) / 16 * s).astype(np.float32),
        "base": (n((K, T2)) * s).astype(np.float32),
        "w1": (n((K, H)) / np.sqrt(K) / s).astype(np.float32),
        "decay": (-0.7 * np.exp(0.3 * n(H))).astype(np.float32),
        "gain": (np.exp(0.3 * n(H)) * u[:, 0]).astype(np.float32),
        "w4_words": w4_words, "w4_scales": w4_scales,
        "bias": (0.3 * n(N)).astype(np.float32),
    }

def reference(tab_words, tab_scales, offs, offs2, offs3, xs, base, w1, decay, gain, w4_words, w4_scales, bias):
    v = unpack_weight(tab_words, tab_scales, "e4m3")[:, unstriped(offs)]
    page = f64(base).copy()
    page[:, unstriped(offs2)] = f64(xs)
    w1q = mxq(f64(w1), 0, "e4m3")
    a = w1q.T @ mxq(page, 0, "e4m3")
    b = w1q.T @ v
    d = np.abs(a[:, unstriped(offs3)] - b)
    z = f64(gain)[:, None] * np.exp(f64(decay)[:, None] * d)
    w4 = unpack_weight(w4_words, w4_scales, "e2m1")
    return (w4.T @ mxq(z, 0, "e4m3")) + f64(bias)[:, None]

@@ -1,0 +1,283 @@
+from contextlib import ExitStack
+
+import concourse.mybir as mybir
+
+K, T, S, H, N = 1024, 2048, 1024, 512, 256
+FLOPS = 2 * K * H * T + 2 * K * H * S + 2 * H * N * S
+
+F32 = mybir.dt.float32
+BF16 = mybir.dt.bfloat16
+I32 = mybir.dt.int32
+U32 = mybir.dt.uint32
+U16 = mybir.dt.uint16
+U8 = mybir.dt.uint8
+FP8X4 = mybir.dt.float8_e4m3fn_x4
+FP4X4 = mybir.dt.float4_e2m1fn_x4
+ACT = mybir.ActivationFunctionType
+ALU = mybir.AluOpType
+
+P = 128
+PACK = 4
+K_PASS = P * PACK
+BANK = 512
+LIST_COLS = S // 16
+
+
+def tile_list_mine_loop_closure_kernel(
+    tc, tab_words, tab_scales, offs, offs2, offs3, xs, base, w1, decay, gain, w4_words, w4_scales, bias, out
+):
+    nc = tc.nc
+    with ExitStack() as ctx:
+        lists = ctx.enter_context(tc.tile_pool(name="lists", bufs=1))
+        sb = ctx.enter_context(tc.tile_pool(name="sb", bufs=1))
+        psum = ctx.enter_context(tc.psum_pool(name="psum", bufs=1))
+
+        def sbuf(shape, dtype, name, tag=None):
+            return sb.tile(shape, dtype, name=name, tag=tag or name, align_bytes=64)
+
+        tab_list = lists.tile([P, LIST_COLS], U16, name="tab_list")
+        slot_list = lists.tile([P, LIST_COLS], U16, name="slot_list")
+        pair_list = lists.tile([P, LIST_COLS], U16, name="pair_list")
+        tab_sc = sbuf([P, T], U8, "tab_sc")
+        nc.vector.memset(tab_sc[:].bitcast(I32), 0)
+        w4_sc = sbuf([P, N], U8, "w4_sc")
+        nc.vector.memset(w4_sc[:].bitcast(I32), 0)
+        nc.sync.dma_start(slot_list[:], offs2)
+
+        planes, news = [], []
+
+        def load_plane(n):
+            a, i = divmod(n, PACK)
+            rows = slice(a * K_PASS, (a + 1) * K_PASS)
+            plane = sbuf([P, T], F32, "plane%d" % n)
+            new = sbuf([P, S], F32, "new%d" % n)
+            nc.sync.dma_start(plane[:], base[rows, :].rearrange("(p i) t -> p i t", i=PACK)[:, i, :])
+            nc.sync.dma_start(new[:], xs[rows, :].rearrange("(p i) m -> p i m", i=PACK)[:, i, :])
+            planes.append(plane)
+            news.append(new)
+
+        load_plane(0)
+        load_plane(1)
+        w1_raw = []
+        for a in range(2):
+            raw = sbuf([P, PACK, H], F32, "w1_raw%d" % a)
+            nc.sync.dma_start(raw[:], w1[a * K_PASS : (a + 1) * K_PASS, :].rearrange("(p j) r -> p j r", j=PACK))
+            w1_raw.append(raw)
+        for n in range(2, 6):
+            load_plane(n)
+        nc.sync.dma_start(tab_list[:], offs)
+        for q in range(4):
+            nc.sync.dma_start(
+                tab_sc[32 * q : 32 * q + 8, :].bitcast(I32), tab_scales[:, 4 * q : 4 * q + 4, :].bitcast(I32)
+            )
+        tab = []
+        for a in range(2):
+            words = sbuf([P, T], I32, "tab%d" % a)
+            nc.sync.dma_start(words[:], tab_words[a].rearrange("p t i -> p (t i)").bitcast(I32))
+            tab.append(words)
+        load_plane(6)
+        load_plane(7)
+        nc.sync.dma_start(pair_list[:], offs3)
+        decay_sb = sbuf([P, PACK], F32, "decay_sb")
+        gain_sb = sbuf([P, PACK], F32, "gain_sb")
+        bias_sb = sbuf([P, 2], F32, "bias_sb")
+        w4 = sbuf([P, 2 * N], U8, "w4")
+        nc.sync.dma_start(decay_sb[:], decay.rearrange("(p t) -> p t", t=PACK))
+        nc.sync.dma_start(gain_sb[:], gain.rearrange("(p t) -> p t", t=PACK))
+        with nc.allow_non_contiguous_dma(reason="one bias value a partition"):
+            nc.sync.dma_start(bias_sb[:], bias.rearrange("(u p) -> p u", p=P))
+        nc.sync.dma_start(w4[:].bitcast(I32), w4_words[0].bitcast(I32))
+        for q in range(4):
+            nc.sync.dma_start(
+                w4_sc[32 * q : 32 * q + 4, :].bitcast(I32), w4_scales[0, 4 * q : 4 * q + 4, :].bitcast(I32)
+            )
+
+        def scatter(n):
+            nc.vector.tensor_copy(planes[n][:].indirect(slot_list[:]), news[n][:])
+
+        HALF = T // 2
+        pairs = [sbuf([P, 2, HALF, 2], BF16, "pairs%d" % h) for h in range(2)]
+
+        def cast_into_pair(n):
+            for h in range(2):
+                nc.scalar.activation(pairs[h][:, n // 2, :, n % 2], planes[n][:, h * HALF : (h + 1) * HALF], ACT.Copy)
+
+        woven1 = [sbuf([P, BANK, PACK], BF16, "woven1_%d" % c) for c in range(4)]
+
+        def cast_into_words(n, c):
+            nc.scalar.activation(woven1[c][:, :, n - PACK], planes[n][:, c * BANK : (c + 1) * BANK], ACT.Copy)
+
+        scatter(0)
+        cast_into_pair(0)
+        w1_bf = sbuf([P, 2, PACK * H], BF16, "w1_bf")
+        for a in range(2):
+            nc.scalar.activation(
+                w1_bf[:, a, :].rearrange("p (t m j) -> p m j t", t=PACK, j=PACK),
+                w1_raw[a][:].rearrange("p j (m t) -> p m j t", t=PACK),
+                ACT.Copy,
+            )
+        for n in range(1, 4):
+            scatter(n)
+            cast_into_pair(n)
+        w1_codes = sbuf([P, 2 * H], U32, "w1_codes", "new3")
+        w1_sc = sbuf([P, 2 * H], U8, "w1_sc")
+        nc.vector.quantize_mx(
+            out=w1_codes[:].bitcast(FP8X4), scales=w1_sc[:], in_=w1_bf[:].rearrange("p a c -> p (a c)")
+        )
+        woven0 = []
+        for h in range(2):
+            woven = sbuf([P, HALF * PACK], BF16, "woven0_%d" % h)
+            nc.scalar.copy(
+                woven[:].bitcast(F32).rearrange("p (c u) -> p c u", u=2),
+                pairs[h][:].rearrange("p u c e -> p u (c e)").bitcast(F32).rearrange("p u c -> p c u"),
+            )
+            woven0.append(woven)
+        page0_codes, page0_sc = [], []
+
+        def quantise0(h):
+            codes = sbuf([P, HALF], U32, "page0_codes%d" % h, "new%d" % (5 + h))
+            scales = sbuf([P, HALF], U8, "page0_sc%d" % h)
+            nc.vector.quantize_mx(out=codes[:].bitcast(FP8X4), scales=scales[:], in_=woven0[h][:])
+            page0_codes.append(codes)
+            page0_sc.append(scales)
+
+        for n in range(4, 8):
+            scatter(n)
+            if n in (5, 6):
+                quantise0(n - 5)
+            for c in range(4):
+                cast_into_words(n, c)
+
+        v_words, page1_codes, page1_sc = [], [], []
+
+        def gather_words(a, tag):
+            words = sbuf([P, S], U32, "v_words%d" % a, tag)
+            nc.vector.tensor_copy(words[:], tab[a][:].bitcast(U32).indirect(tab_list[:]))
+            v_words.append(words)
+
+        def quantise1(c):
+            codes = sbuf([P, BANK], U32, "page1_codes%d" % c)
+            scales = sbuf([P, BANK], U8, "page1_sc%d" % c)
+            nc.vector.quantize_mx(
+                out=codes[:].bitcast(FP8X4), scales=scales[:], in_=woven1[c][:].rearrange("p c i -> p (c i)")
+            )
+            page1_codes.append(codes)
+            page1_sc.append(scales)
+
+        gather_words(0, "new7")
+        quantise1(0)
+        gather_words(1, "woven1_0")
+        for c in range(1, 4):
+            quantise1(c)
+        v_sc = sbuf([P, S], U8, "v_sc", "woven1_3")
+        nc.vector.tensor_copy(v_sc[:], tab_sc[:].indirect(tab_list[:]))
+
+        def project(acc, t, moving):
+            for a in range(2):
+                cols = slice(a * H + t * P, a * H + (t + 1) * P)
+                codes, scales = moving[a]
+                nc.tensor.matmul_mx(
+                    out=acc[:],
+                    lhsT=w1_codes[:, cols].bitcast(FP8X4),
+                    lhsT_scale=w1_sc[:, cols],
+                    rhs=codes.bitcast(FP8X4),
+                    rhs_scale=scales,
+                    start=(a == 0),
+                    stop=(a == 1),
+                )
+
+        a_sb = [sbuf([P, T], F32, "a%d" % t, "plane%d" % t) for t in range(PACK)]
+
+        def project_page(t, c):
+            acc = psum.tile([P, BANK], F32, name="acc", tag="acc", bufs=8)
+            h, cols = c // 2, slice((c % 2) * BANK, (c % 2 + 1) * BANK)
+            project(acc, t, [(page0_codes[h][:, cols], page0_sc[h][:, cols]), (page1_codes[c][:], page1_sc[c][:])])
+            return acc
+
+        def store_a(t, c, acc, on_vector=False):
+            if on_vector:
+                nc.vector.tensor_copy(a_sb[t][:, c * BANK : (c + 1) * BANK], acc[:])
+            else:
+                nc.scalar.activation(a_sb[t][:, c * BANK : (c + 1) * BANK], acc[:], ACT.Copy)
+
+        dist = [sbuf([P, PACK, BANK], F32, "dist%d" % h, "pairs%d" % h) for h in range(2)]
+
+        def gather_a(t, h):
+            half = slice(h * LIST_COLS // 2, (h + 1) * LIST_COLS // 2)
+            picked = sb.tile([P, BANK], F32, name="picked", tag="picked", bufs=2, align_bytes=64)
+            nc.vector.tensor_copy(picked[:], a_sb[t][:].indirect(pair_list[:, half]))
+            return picked
+
+        def subtract_b(t, h, picked):
+            acc = psum.tile([P, BANK], F32, name="acc", tag="acc", bufs=8)
+            cols = slice(h * BANK, (h + 1) * BANK)
+            project(acc, t, [(v_words[a][:, cols], v_sc[4 * a :, cols]) for a in range(2)])
+            nc.vector.tensor_tensor(dist[h][:, t, :], picked[:], acc[:], ALU.subtract)
+            nc.scalar.activation(dist[h][:, t, :], dist[h][:, t, :], ACT.Abs, scale=decay_sb[:, t : t + 1])
+
+        def similarity(n, j0, width, tag):
+            h, c0 = divmod(j0, BANK)
+            sim = sbuf([P, width, PACK], F32, "sim%d" % n, tag)
+            nc.scalar.activation(
+                sim[:].rearrange("p (c i) t -> p c t i", i=4),
+                dist[h][:, :, c0 : c0 + width].rearrange("p t (c i) -> p c t i", i=4),
+                ACT.Exp,
+                scale=-1.0,
+            )
+            return sim
+
+        def weigh(n, sim, width, tag):
+            z = sbuf([P, width, PACK], BF16, "z%d" % n, tag)
+            nc.vector.tensor_tensor(z[:], sim[:], gain_sb[:].unsqueeze(1).to_broadcast([P, width, PACK]), ALU.mult)
+            return z
+
+        def votes(n, z, j0, width):
+            codes = sbuf([P, width], U32, "z_codes%d" % n)
+            scales = sbuf([P, width], U8, "z_sc%d" % n)
+            nc.vector.quantize_mx(out=codes[:].bitcast(FP8X4), scales=scales[:], in_=z[:].rearrange("p c t -> p (c t)"))
+            for u in range(2):
+                acc = psum.tile([P, BANK], F32, name="acc", tag="acc", bufs=8)
+                nc.tensor.matmul_mx(
+                    out=acc[:, :width],
+                    lhsT=w4[:, 2 * P * u : 2 * P * (u + 1)].bitcast(FP4X4),
+                    lhsT_scale=w4_sc[:, P * u : P * (u + 1)],
+                    rhs=codes[:].bitcast(FP8X4),
+                    rhs_scale=scales[:],
+                    start=True,
+                    stop=True,
+                )
+                res = sbuf([P, width], F32, "res%d_%d" % (n, u))
+                if u == 1 and n == 2:
+                    nc.vector.tensor_scalar(res[:], acc[:, :width], bias_sb[:, u : u + 1], None, ALU.add)
+                else:
+                    nc.scalar.activation(res[:], acc[:, :width], ACT.Identity, bias=bias_sb[:, u : u + 1])
+                (nc.scalar if (u == 0 and n == 2) else nc.sync).dma_start(out[u * P : (u + 1) * P, j0 : j0 + width], res[:])
+
+        first = {}
+        for c in range(4):
+            for t in range(2):
+                first[t, c] = project_page(t, c)
+        for t in range(2):
+            for c in range(4):
+                store_a(t, c, first[t, c])
+        order = [(0, 0), (1, 0), (0, 1), (2, 0), (3, 0), (1, 1), (2, 1), (3, 1)]
+        picked = gather_a(0, 0)
+        for c in range(4):
+            store_a(2, c, project_page(2, c))
+        for n in range(8):
+            ahead = gather_a(*order[n + 1]) if n < 7 else None
+            subtract_b(*order[n], picked)
+            picked = ahead
+            if n == 0:
+                for c in range(4):
+                    store_a(3, c, project_page(3, c))
+            if n == 4:
+                sim0 = similarity(0, 0, BANK, "w1_raw0")
+        sim1 = similarity(1, BANK, BANK // 2, "w1_raw1")
+        sim2 = similarity(2, BANK + BANK // 2, BANK // 2, "new0")
+        z0 = weigh(0, sim0, BANK, "plane3")
+        votes(0, z0, 0, BANK)
+        z1 = weigh(1, sim1, BANK // 2, "new2")
+        z2 = weigh(2, sim2, BANK // 2, "new1")
+        votes(1, z1, BANK, BANK // 2)
+        votes(2, z2, BANK + BANK // 2, BANK // 2)

@@ -42,7 +42,20 @@ def tile_list_mine_loop_closure_kernel(
         nc.vector.memset(tab_sc[:].bitcast(I32), 0)
         w4_sc = sbuf([P, N], U8, "w4_sc")
         nc.vector.memset(w4_sc[:].bitcast(I32), 0)
+        nc.sync.dma_start(tab_list[:], offs)
+        for q in range(4):
+            nc.sync.dma_start(
+                tab_sc[32 * q : 32 * q + 8, :].bitcast(I32), tab_scales[:, 4 * q : 4 * q + 4, :].bitcast(I32)
+            )
         nc.sync.dma_start(slot_list[:], offs2)
+        v_sc = sbuf([P, S], U8, "v_sc")
+        nc.vector.tensor_copy(v_sc[:], tab_sc[:].indirect(tab_list[:]))
+
+        banks = []
+
+        def next_bank():
+            banks.append(psum.tile([P, BANK], F32, name="bank%d" % (len(banks) % 8)))
+            return banks[-1]
 
         planes, news = [], []
 
@@ -52,7 +65,9 @@ def tile_list_mine_loop_closure_kernel(
             plane = sbuf([P, T], F32, "plane%d" % n)
             new = sbuf([P, S], F32, "new%d" % n)
             nc.sync.dma_start(plane[:], base[rows, :].rearrange("(p i) t -> p i t", i=PACK)[:, i, :])
-            nc.sync.dma_start(new[:], xs[rows, :].rearrange("(p i) m -> p i m", i=PACK)[:, i, :])
+            src = xs[rows, :].rearrange("(p i) m -> p i m", i=PACK)[:, i, :]
+            for cols in (slice(0, S // 2), slice(S // 2, S)) if n == 0 else (slice(0, S),):
+                nc.sync.dma_start(new[:, cols], src[:, cols])
             planes.append(plane)
             news.append(new)
 
@@ -65,11 +80,6 @@ def tile_list_mine_loop_closure_kernel(
             w1_raw.append(raw)
         for n in range(2, 6):
             load_plane(n)
-        nc.sync.dma_start(tab_list[:], offs)
-        for q in range(4):
-            nc.sync.dma_start(
-                tab_sc[32 * q : 32 * q + 8, :].bitcast(I32), tab_scales[:, 4 * q : 4 * q + 4, :].bitcast(I32)
-            )
         tab = []
         for a in range(2):
             words = sbuf([P, T], I32, "tab%d" % a)
@@ -100,14 +110,18 @@ def tile_list_mine_loop_closure_kernel(
 
         def cast_into_pair(n):
             for h in range(2):
-                nc.scalar.activation(pairs[h][:, n // 2, :, n % 2], planes[n][:, h * HALF : (h + 1) * HALF], ACT.Copy)
+                nc.scalar.activation(pairs[h][:, n % PACK // 2, :, n % 2], planes[n][:, h * HALF : (h + 1) * HALF], ACT.Copy)
 
         woven1 = [sbuf([P, BANK, PACK], BF16, "woven1_%d" % c) for c in range(4)]
 
         def cast_into_words(n, c):
             nc.scalar.activation(woven1[c][:, :, n - PACK], planes[n][:, c * BANK : (c + 1) * BANK], ACT.Copy)
 
-        scatter(0)
+        for h in range(2):
+            nc.vector.tensor_copy(
+                planes[0][:].indirect(slot_list[:, h * LIST_COLS // 2 : (h + 1) * LIST_COLS // 2]),
+                news[0][:, h * S // 2 : (h + 1) * S // 2],
+            )
         cast_into_pair(0)
         w1_bf = sbuf([P, 2, PACK * H], BF16, "w1_bf")
         for a in range(2):
@@ -119,11 +133,6 @@ def tile_list_mine_loop_closure_kernel(
         for n in range(1, 4):
             scatter(n)
             cast_into_pair(n)
-        w1_codes = sbuf([P, 2 * H], U32, "w1_codes", "new3")
-        w1_sc = sbuf([P, 2 * H], U8, "w1_sc")
-        nc.vector.quantize_mx(
-            out=w1_codes[:].bitcast(FP8X4), scales=w1_sc[:], in_=w1_bf[:].rearrange("p a c -> p (a c)")
-        )
         woven0 = []
         for h in range(2):
             woven = sbuf([P, HALF * PACK], BF16, "woven0_%d" % h)
@@ -134,19 +143,33 @@ def tile_list_mine_loop_closure_kernel(
             woven0.append(woven)
         page0_codes, page0_sc = [], []
 
-        def quantise0(h):
-            codes = sbuf([P, HALF], U32, "page0_codes%d" % h, "new%d" % (5 + h))
+        def quantise0(h, tag):
+            codes = sbuf([P, HALF], U32, "page0_codes%d" % h, tag)
             scales = sbuf([P, HALF], U8, "page0_sc%d" % h)
             nc.vector.quantize_mx(out=codes[:].bitcast(FP8X4), scales=scales[:], in_=woven0[h][:])
             page0_codes.append(codes)
             page0_sc.append(scales)
 
-        for n in range(4, 8):
+        for n in (4, 5):
             scatter(n)
-            if n in (5, 6):
-                quantise0(n - 5)
-            for c in range(4):
-                cast_into_words(n, c)
+            cast_into_pair(n)
+        for c in range(4):
+            cols = slice((c % 2) * BANK, (c % 2 + 1) * BANK)
+            nc.scalar.copy(
+                woven1[c][:].rearrange("p c i -> p (c i)").bitcast(F32).rearrange("p (c u) -> p c u", u=2),
+                pairs[c // 2][:, 0, cols, :].bitcast(F32).to_broadcast([P, BANK, 2]),
+            )
+        scatter(6)
+        for c in range(4):
+            cast_into_words(6, c)
+        w1_codes = sbuf([P, 2 * H], U32, "w1_codes", "new6")
+        w1_sc = sbuf([P, 2 * H], U8, "w1_sc")
+        nc.vector.quantize_mx(
+            out=w1_codes[:].bitcast(FP8X4), scales=w1_sc[:], in_=w1_bf[:].rearrange("p a c -> p (a c)")
+        )
+        scatter(7)
+        for c in range(4):
+            cast_into_words(7, c)
 
         v_words, page1_codes, page1_sc = [], [], []
 
@@ -164,13 +187,14 @@ def tile_list_mine_loop_closure_kernel(
             page1_codes.append(codes)
             page1_sc.append(scales)
 
-        gather_words(0, "new7")
+        quantise0(0, "new7")
+        gather_words(0, "woven0_0")
         quantise1(0)
-        gather_words(1, "woven1_0")
-        for c in range(1, 4):
-            quantise1(c)
-        v_sc = sbuf([P, S], U8, "v_sc", "woven1_3")
-        nc.vector.tensor_copy(v_sc[:], tab_sc[:].indirect(tab_list[:]))
+        quantise1(1)
+        quantise0(1, "woven1_0")
+        quantise1(2)
+        quantise1(3)
+        gather_words(1, "woven1_2")
 
         def project(acc, t, moving):
             for a in range(2):
@@ -186,10 +210,10 @@ def tile_list_mine_loop_closure_kernel(
                     stop=(a == 1),
                 )
 
-        a_sb = [sbuf([P, T], F32, "a%d" % t, "plane%d" % t) for t in range(PACK)]
+        a_sb = [sbuf([P, T], F32, "a%d" % t, ("woven1_3", "tab1", "plane2", "plane3")[t]) for t in range(PACK)]
 
         def project_page(t, c):
-            acc = psum.tile([P, BANK], F32, name="acc", tag="acc", bufs=8)
+            acc = next_bank()
             h, cols = c // 2, slice((c % 2) * BANK, (c % 2 + 1) * BANK)
             project(acc, t, [(page0_codes[h][:, cols], page0_sc[h][:, cols]), (page1_codes[c][:], page1_sc[c][:])])
             return acc
@@ -209,7 +233,7 @@ def tile_list_mine_loop_closure_kernel(
             return picked
 
         def subtract_b(t, h, picked):
-            acc = psum.tile([P, BANK], F32, name="acc", tag="acc", bufs=8)
+            acc = next_bank()
             cols = slice(h * BANK, (h + 1) * BANK)
             project(acc, t, [(v_words[a][:, cols], v_sc[4 * a :, cols]) for a in range(2)])
             nc.vector.tensor_tensor(dist[h][:, t, :], picked[:], acc[:], ALU.subtract)
@@ -236,7 +260,7 @@ def tile_list_mine_loop_closure_kernel(
             scales = sbuf([P, width], U8, "z_sc%d" % n)
             nc.vector.quantize_mx(out=codes[:].bitcast(FP8X4), scales=scales[:], in_=z[:].rearrange("p c t -> p (c t)"))
             for u in range(2):
-                acc = psum.tile([P, BANK], F32, name="acc", tag="acc", bufs=8)
+                acc = next_bank()
                 nc.tensor.matmul_mx(
                     out=acc[:, :width],
                     lhsT=w4[:, 2 * P * u : 2 * P * (u + 1)].bitcast(FP4X4),
@@ -253,14 +277,10 @@ def tile_list_mine_loop_closure_kernel(
                     nc.scalar.activation(res[:], acc[:, :width], ACT.Identity, bias=bias_sb[:, u : u + 1])
                 (nc.scalar if (u == 0 and n == 2) else nc.sync).dma_start(out[u * P : (u + 1) * P, j0 : j0 + width], res[:])
 
-        first = {}
-        for c in range(4):
-            for t in range(2):
-                first[t, c] = project_page(t, c)
         for t in range(2):
             for c in range(4):
-                store_a(t, c, first[t, c])
-        order = [(0, 0), (1, 0), (0, 1), (2, 0), (3, 0), (1, 1), (2, 1), (3, 1)]
+                store_a(t, c, project_page(t, c))
+        order = [(0, 0), (0, 1), (1, 0), (2, 0), (3, 0), (1, 1), (2, 1), (3, 1)]
         picked = gather_a(0, 0)
         for c in range(4):
             store_a(2, c, project_page(2, c))

@@ -83,10 +83,12 @@ def tile_list_mine_loop_closure_kernel(
         tab = []
         for a in range(2):
             words = sbuf([P, T], I32, "tab%d" % a)
-            nc.sync.dma_start(words[:], tab_words[a].rearrange("p t i -> p (t i)").bitcast(I32))
+            cols = slice(0, T - 128 if a == 0 else T)
+            nc.sync.dma_start(words[:, cols], tab_words[a].rearrange("p t i -> p (t i)").bitcast(I32)[:, cols])
             tab.append(words)
         load_plane(6)
         load_plane(7)
+        nc.sync.dma_start(tab[0][:, T - 128 :], tab_words[0].rearrange("p t i -> p (t i)").bitcast(I32)[:, T - 128 :])
         nc.sync.dma_start(pair_list[:], offs3)
         decay_sb = sbuf([P, PACK], F32, "decay_sb")
         gain_sb = sbuf([P, PACK], F32, "gain_sb")
@@ -162,11 +164,6 @@ def tile_list_mine_loop_closure_kernel(
         scatter(6)
         for c in range(4):
             cast_into_words(6, c)
-        w1_codes = sbuf([P, 2 * H], U32, "w1_codes", "new6")
-        w1_sc = sbuf([P, 2 * H], U8, "w1_sc")
-        nc.vector.quantize_mx(
-            out=w1_codes[:].bitcast(FP8X4), scales=w1_sc[:], in_=w1_bf[:].rearrange("p a c -> p (a c)")
-        )
         scatter(7)
         for c in range(4):
             cast_into_words(7, c)
@@ -187,9 +184,14 @@ def tile_list_mine_loop_closure_kernel(
             page1_codes.append(codes)
             page1_sc.append(scales)
 
+        gather_words(0, None)
         quantise0(0, "new7")
-        gather_words(0, "woven0_0")
         quantise1(0)
+        w1_codes = sbuf([P, 2 * H], U32, "w1_codes", "woven0_0")
+        w1_sc = sbuf([P, 2 * H], U8, "w1_sc")
+        nc.vector.quantize_mx(
+            out=w1_codes[:].bitcast(FP8X4), scales=w1_sc[:], in_=w1_bf[:].rearrange("p a c -> p (a c)")
+        )
         quantise1(1)
         quantise0(1, "woven1_0")
         quantise1(2)
@@ -237,14 +239,18 @@ def tile_list_mine_loop_closure_kernel(
             cols = slice(h * BANK, (h + 1) * BANK)
             project(acc, t, [(v_words[a][:, cols], v_sc[4 * a :, cols]) for a in range(2)])
             nc.vector.tensor_tensor(dist[h][:, t, :], picked[:], acc[:], ALU.subtract)
-            nc.scalar.activation(dist[h][:, t, :], dist[h][:, t, :], ACT.Abs, scale=decay_sb[:, t : t + 1])
+
+        rate = [sbuf([P, PACK, BANK], F32, "rate%d" % h, ("page1_codes3", "woven1_0")[h]) for h in range(2)]
+
+        def scale_distance(t, h):
+            nc.scalar.activation(rate[h][:, t, :], dist[h][:, t, :], ACT.Abs, scale=decay_sb[:, t : t + 1])
 
         def similarity(n, j0, width, tag):
             h, c0 = divmod(j0, BANK)
             sim = sbuf([P, width, PACK], F32, "sim%d" % n, tag)
             nc.scalar.activation(
                 sim[:].rearrange("p (c i) t -> p c t i", i=4),
-                dist[h][:, :, c0 : c0 + width].rearrange("p t (c i) -> p c t i", i=4),
+                rate[h][:, :, c0 : c0 + width].rearrange("p t (c i) -> p c t i", i=4),
                 ACT.Exp,
                 scale=-1.0,
             )
@@ -256,7 +262,7 @@ def tile_list_mine_loop_closure_kernel(
             return z
 
         def votes(n, z, j0, width):
-            codes = sbuf([P, width], U32, "z_codes%d" % n)
+            codes = sbuf([P, width], U32, "z_codes%d" % n, "woven1_0" if n == 1 else None)
             scales = sbuf([P, width], U8, "z_sc%d" % n)
             nc.vector.quantize_mx(out=codes[:].bitcast(FP8X4), scales=scales[:], in_=z[:].rearrange("p c t -> p (c t)"))
             for u in range(2):
@@ -270,34 +276,38 @@ def tile_list_mine_loop_closure_kernel(
                     start=True,
                     stop=True,
                 )
-                res = sbuf([P, width], F32, "res%d_%d" % (n, u))
+                res = sbuf([P, width], F32, "res%d_%d" % (n, u), "plane%d" % (4 + u) if n == 0 else None)
                 if u == 1 and n == 2:
                     nc.vector.tensor_scalar(res[:], acc[:, :width], bias_sb[:, u : u + 1], None, ALU.add)
                 else:
                     nc.scalar.activation(res[:], acc[:, :width], ACT.Identity, bias=bias_sb[:, u : u + 1])
                 (nc.scalar if (u == 0 and n == 2) else nc.sync).dma_start(out[u * P : (u + 1) * P, j0 : j0 + width], res[:])
 
+        def compare(first, second):
+            picked = [gather_a(*first), gather_a(*second)]
+            subtract_b(*first, picked[0])
+            subtract_b(*second, picked[1])
+
         for t in range(2):
             for c in range(4):
                 store_a(t, c, project_page(t, c))
-        order = [(0, 0), (0, 1), (1, 0), (2, 0), (3, 0), (1, 1), (2, 1), (3, 1)]
-        picked = gather_a(0, 0)
+        compare((0, 0), (0, 1))
         for c in range(4):
-            store_a(2, c, project_page(2, c))
-        for n in range(8):
-            ahead = gather_a(*order[n + 1]) if n < 7 else None
-            subtract_b(*order[n], picked)
-            picked = ahead
-            if n == 0:
-                for c in range(4):
-                    store_a(3, c, project_page(3, c))
-            if n == 4:
-                sim0 = similarity(0, 0, BANK, "w1_raw0")
+            for t in (2, 3):
+                store_a(t, c, project_page(t, c))
+        compare((1, 0), (1, 1))
+        compare((2, 0), (3, 0))
+        compare((2, 1), (3, 1))
+        for t in range(4):
+            scale_distance(t, 0)
+        sim0 = similarity(0, 0, BANK, "w1_raw0")
+        for t in range(4):
+            scale_distance(t, 1)
         sim1 = similarity(1, BANK, BANK // 2, "w1_raw1")
         sim2 = similarity(2, BANK + BANK // 2, BANK // 2, "new0")
         z0 = weigh(0, sim0, BANK, "plane3")
-        votes(0, z0, 0, BANK)
         z1 = weigh(1, sim1, BANK // 2, "new2")
+        votes(0, z0, 0, BANK)
         z2 = weigh(2, sim2, BANK // 2, "new1")
         votes(1, z1, BANK, BANK // 2)
         votes(2, z2, BANK + BANK // 2, BANK // 2)

@@ -19,8 +19,15 @@ ALU = mybir.AluOpType
 P = 128
 PACK = 4
 K_PASS = P * PACK
+PASSES = K // K_PASS
+QUADRANTS = 4
 BANK = 512
+PSUM_BANKS = 8
+CHUNKS = T // BANK
+PAGE_HALF = T // 2
 LIST_COLS = S // 16
+LINE = 4
+TAB_TAIL = 128
 
 
 def tile_list_mine_loop_closure_kernel(
@@ -35,6 +42,15 @@ def tile_list_mine_loop_closure_kernel(
         def sbuf(shape, dtype, name, tag=None):
             return sb.tile(shape, dtype, name=name, tag=tag or name, align_bytes=64)
 
+        banks = []
+
+        def next_bank():
+            banks.append(psum.tile([P, BANK], F32, name="bank%d" % (len(banks) % PSUM_BANKS)))
+            return banks[-1]
+
+        def list_half(tile, h):
+            return tile[:, h * LIST_COLS // 2 : (h + 1) * LIST_COLS // 2]
+
         tab_list = lists.tile([P, LIST_COLS], U16, name="tab_list")
         slot_list = lists.tile([P, LIST_COLS], U16, name="slot_list")
         pair_list = lists.tile([P, LIST_COLS], U16, name="pair_list")
@@ -43,63 +59,58 @@ def tile_list_mine_loop_closure_kernel(
         w4_sc = sbuf([P, N], U8, "w4_sc")
         nc.vector.memset(w4_sc[:].bitcast(I32), 0)
         nc.sync.dma_start(tab_list[:], offs)
-        for q in range(4):
+        for q in range(QUADRANTS):
             nc.sync.dma_start(
-                tab_sc[32 * q : 32 * q + 8, :].bitcast(I32), tab_scales[:, 4 * q : 4 * q + 4, :].bitcast(I32)
+                tab_sc[32 * q : 32 * q + 4 * PASSES, :].bitcast(I32), tab_scales[:, 4 * q : 4 * q + 4, :].bitcast(I32)
             )
         nc.sync.dma_start(slot_list[:], offs2)
         v_sc = sbuf([P, S], U8, "v_sc")
         nc.vector.tensor_copy(v_sc[:], tab_sc[:].indirect(tab_list[:]))
 
-        banks = []
-
-        def next_bank():
-            banks.append(psum.tile([P, BANK], F32, name="bank%d" % (len(banks) % 8)))
-            return banks[-1]
-
         planes, news = [], []
 
-        def load_plane(n):
-            a, i = divmod(n, PACK)
-            rows = slice(a * K_PASS, (a + 1) * K_PASS)
+        def load_plane(n, pieces):
+            g, i = divmod(n, PACK)
+            rows = slice(g * K_PASS, (g + 1) * K_PASS)
             plane = sbuf([P, T], F32, "plane%d" % n)
             new = sbuf([P, S], F32, "new%d" % n)
             nc.sync.dma_start(plane[:], base[rows, :].rearrange("(p i) t -> p i t", i=PACK)[:, i, :])
-            src = xs[rows, :].rearrange("(p i) m -> p i m", i=PACK)[:, i, :]
-            for cols in (slice(0, S // 2), slice(S // 2, S)) if n == 0 else (slice(0, S),):
-                nc.sync.dma_start(new[:, cols], src[:, cols])
+            xs_rows = xs[rows, :].rearrange("(p i) m -> p i m", i=PACK)[:, i, :]
+            for piece in range(pieces):
+                cols = slice(piece * S // pieces, (piece + 1) * S // pieces)
+                nc.sync.dma_start(new[:, cols], xs_rows[:, cols])
             planes.append(plane)
             news.append(new)
 
-        load_plane(0)
-        load_plane(1)
+        load_plane(0, 2)
+        load_plane(1, 1)
         w1_raw = []
-        for a in range(2):
-            raw = sbuf([P, PACK, H], F32, "w1_raw%d" % a)
-            nc.sync.dma_start(raw[:], w1[a * K_PASS : (a + 1) * K_PASS, :].rearrange("(p j) r -> p j r", j=PACK))
+        for g in range(PASSES):
+            raw = sbuf([P, PACK, H], F32, "w1_raw%d" % g)
+            nc.sync.dma_start(raw[:], w1[g * K_PASS : (g + 1) * K_PASS, :].rearrange("(p i) r -> p i r", i=PACK))
             w1_raw.append(raw)
         for n in range(2, 6):
-            load_plane(n)
+            load_plane(n, 1)
+        tab_hbm = [tab_words[g].rearrange("p t i -> p (t i)").bitcast(I32) for g in range(PASSES)]
         tab = []
-        for a in range(2):
-            words = sbuf([P, T], I32, "tab%d" % a)
-            cols = slice(0, T - 128 if a == 0 else T)
-            nc.sync.dma_start(words[:, cols], tab_words[a].rearrange("p t i -> p (t i)").bitcast(I32)[:, cols])
+        for g, early_cols in enumerate((T - TAB_TAIL, T)):
+            words = sbuf([P, T], I32, "tab%d" % g)
+            nc.sync.dma_start(words[:, :early_cols], tab_hbm[g][:, :early_cols])
             tab.append(words)
-        load_plane(6)
-        load_plane(7)
-        nc.sync.dma_start(tab[0][:, T - 128 :], tab_words[0].rearrange("p t i -> p (t i)").bitcast(I32)[:, T - 128 :])
+        load_plane(6, 1)
+        load_plane(7, 1)
+        nc.sync.dma_start(tab[0][:, T - TAB_TAIL :], tab_hbm[0][:, T - TAB_TAIL :])
         nc.sync.dma_start(pair_list[:], offs3)
         decay_sb = sbuf([P, PACK], F32, "decay_sb")
         gain_sb = sbuf([P, PACK], F32, "gain_sb")
-        bias_sb = sbuf([P, 2], F32, "bias_sb")
+        bias_sb = sbuf([P, N // P], F32, "bias_sb")
         w4 = sbuf([P, 2 * N], U8, "w4")
         nc.sync.dma_start(decay_sb[:], decay.rearrange("(p t) -> p t", t=PACK))
         nc.sync.dma_start(gain_sb[:], gain.rearrange("(p t) -> p t", t=PACK))
         with nc.allow_non_contiguous_dma(reason="one bias value a partition"):
             nc.sync.dma_start(bias_sb[:], bias.rearrange("(u p) -> p u", p=P))
         nc.sync.dma_start(w4[:].bitcast(I32), w4_words[0].bitcast(I32))
-        for q in range(4):
+        for q in range(QUADRANTS):
             nc.sync.dma_start(
                 w4_sc[32 * q : 32 * q + 4, :].bitcast(I32), w4_scales[0, 4 * q : 4 * q + 4, :].bitcast(I32)
             )
@@ -107,75 +118,64 @@ def tile_list_mine_loop_closure_kernel(
         def scatter(n):
             nc.vector.tensor_copy(planes[n][:].indirect(slot_list[:]), news[n][:])
 
-        HALF = T // 2
-        pairs = [sbuf([P, 2, HALF, 2], BF16, "pairs%d" % h) for h in range(2)]
+        pairs = [sbuf([P, 2, PAGE_HALF, 2], BF16, "pairs%d" % h) for h in range(2)]
 
-        def cast_into_pair(n):
+        def round_into_pairs(n):
+            u, e = divmod(n % PACK, 2)
             for h in range(2):
-                nc.scalar.activation(pairs[h][:, n % PACK // 2, :, n % 2], planes[n][:, h * HALF : (h + 1) * HALF], ACT.Copy)
+                nc.scalar.activation(pairs[h][:, u, :, e], planes[n][:, h * PAGE_HALF : (h + 1) * PAGE_HALF], ACT.Copy)
 
-        woven1 = [sbuf([P, BANK, PACK], BF16, "woven1_%d" % c) for c in range(4)]
+        woven1 = [sbuf([P, BANK, PACK], BF16, "woven1_%d" % c) for c in range(CHUNKS)]
 
-        def cast_into_words(n, c):
-            nc.scalar.activation(woven1[c][:, :, n - PACK], planes[n][:, c * BANK : (c + 1) * BANK], ACT.Copy)
+        def round_into_words(n):
+            for c in range(CHUNKS):
+                nc.scalar.activation(woven1[c][:, :, n - PACK], planes[n][:, c * BANK : (c + 1) * BANK], ACT.Copy)
 
         for h in range(2):
-            nc.vector.tensor_copy(
-                planes[0][:].indirect(slot_list[:, h * LIST_COLS // 2 : (h + 1) * LIST_COLS // 2]),
-                news[0][:, h * S // 2 : (h + 1) * S // 2],
-            )
-        cast_into_pair(0)
-        w1_bf = sbuf([P, 2, PACK * H], BF16, "w1_bf")
-        for a in range(2):
+            nc.vector.tensor_copy(planes[0][:].indirect(list_half(slot_list, h)), news[0][:, h * S // 2 : (h + 1) * S // 2])
+        round_into_pairs(0)
+        w1_woven = sbuf([P, PASSES, PACK * H], BF16, "w1_bf")
+        for g in range(PASSES):
             nc.scalar.activation(
-                w1_bf[:, a, :].rearrange("p (t m j) -> p m j t", t=PACK, j=PACK),
-                w1_raw[a][:].rearrange("p j (m t) -> p m j t", t=PACK),
+                w1_woven[:, g, :].rearrange("p (t m i) -> p m i t", t=PACK, i=PACK),
+                w1_raw[g][:].rearrange("p i (m t) -> p m i t", t=PACK),
                 ACT.Copy,
             )
-        for n in range(1, 4):
+        for n in range(1, PACK):
             scatter(n)
-            cast_into_pair(n)
+            round_into_pairs(n)
         woven0 = []
         for h in range(2):
-            woven = sbuf([P, HALF * PACK], BF16, "woven0_%d" % h)
+            woven = sbuf([P, PAGE_HALF * PACK], BF16, "woven0_%d" % h)
             nc.scalar.copy(
                 woven[:].bitcast(F32).rearrange("p (c u) -> p c u", u=2),
                 pairs[h][:].rearrange("p u c e -> p u (c e)").bitcast(F32).rearrange("p u c -> p c u"),
             )
             woven0.append(woven)
-        page0_codes, page0_sc = [], []
 
-        def quantise0(h, tag):
-            codes = sbuf([P, HALF], U32, "page0_codes%d" % h, tag)
-            scales = sbuf([P, HALF], U8, "page0_sc%d" % h)
+        for n in (4, 5):
+            scatter(n)
+            round_into_pairs(n)
+        for c in range(CHUNKS):
+            h, part = divmod(c, 2)
+            nc.scalar.copy(
+                woven1[c][:].rearrange("p c i -> p (c i)").bitcast(F32).rearrange("p (c u) -> p c u", u=2),
+                pairs[h][:, 0, part * BANK : (part + 1) * BANK, :].bitcast(F32).to_broadcast([P, BANK, 2]),
+            )
+        for n in (6, 7):
+            scatter(n)
+            round_into_words(n)
+
+        page0_codes, page0_sc, page1_codes, page1_sc, v_words = [], [], [], [], []
+
+        def quantise_pass0(h, tag):
+            codes = sbuf([P, PAGE_HALF], U32, "page0_codes%d" % h, tag)
+            scales = sbuf([P, PAGE_HALF], U8, "page0_sc%d" % h)
             nc.vector.quantize_mx(out=codes[:].bitcast(FP8X4), scales=scales[:], in_=woven0[h][:])
             page0_codes.append(codes)
             page0_sc.append(scales)
 
-        for n in (4, 5):
-            scatter(n)
-            cast_into_pair(n)
-        for c in range(4):
-            cols = slice((c % 2) * BANK, (c % 2 + 1) * BANK)
-            nc.scalar.copy(
-                woven1[c][:].rearrange("p c i -> p (c i)").bitcast(F32).rearrange("p (c u) -> p c u", u=2),
-                pairs[c // 2][:, 0, cols, :].bitcast(F32).to_broadcast([P, BANK, 2]),
-            )
-        scatter(6)
-        for c in range(4):
-            cast_into_words(6, c)
-        scatter(7)
-        for c in range(4):
-            cast_into_words(7, c)
-
-        v_words, page1_codes, page1_sc = [], [], []
-
-        def gather_words(a, tag):
-            words = sbuf([P, S], U32, "v_words%d" % a, tag)
-            nc.vector.tensor_copy(words[:], tab[a][:].bitcast(U32).indirect(tab_list[:]))
-            v_words.append(words)
-
-        def quantise1(c):
+        def quantise_pass1(c):
             codes = sbuf([P, BANK], U32, "page1_codes%d" % c)
             scales = sbuf([P, BANK], U8, "page1_sc%d" % c)
             nc.vector.quantize_mx(
@@ -184,73 +184,79 @@ def tile_list_mine_loop_closure_kernel(
             page1_codes.append(codes)
             page1_sc.append(scales)
 
-        gather_words(0, None)
-        quantise0(0, "new7")
-        quantise1(0)
-        w1_codes = sbuf([P, 2 * H], U32, "w1_codes", "woven0_0")
-        w1_sc = sbuf([P, 2 * H], U8, "w1_sc")
+        def gather_words(g, tag):
+            words = sbuf([P, S], U32, "v_words%d" % g, tag)
+            nc.vector.tensor_copy(words[:], tab[g][:].bitcast(U32).indirect(tab_list[:]))
+            v_words.append(words)
+
+        gather_words(0, "v_words0")
+        quantise_pass0(0, "new7")
+        quantise_pass1(0)
+        w1_codes = sbuf([P, PASSES * H], U32, "w1_codes", "woven0_0")
+        w1_sc = sbuf([P, PASSES * H], U8, "w1_sc")
         nc.vector.quantize_mx(
-            out=w1_codes[:].bitcast(FP8X4), scales=w1_sc[:], in_=w1_bf[:].rearrange("p a c -> p (a c)")
+            out=w1_codes[:].bitcast(FP8X4), scales=w1_sc[:], in_=w1_woven[:].rearrange("p g c -> p (g c)")
         )
-        quantise1(1)
-        quantise0(1, "woven1_0")
-        quantise1(2)
-        quantise1(3)
-        gather_words(1, "woven1_2")
+        quantise_pass1(1)
+        quantise_pass0(1, "woven1_0")
+        quantise_pass1(2)
+        quantise_pass1(3)
+        gather_words(1, "woven1_1")
 
         def project(acc, t, moving):
-            for a in range(2):
-                cols = slice(a * H + t * P, a * H + (t + 1) * P)
-                codes, scales = moving[a]
+            for g in range(PASSES):
+                cols = slice(g * H + t * P, g * H + (t + 1) * P)
+                codes, scales = moving[g]
                 nc.tensor.matmul_mx(
                     out=acc[:],
                     lhsT=w1_codes[:, cols].bitcast(FP8X4),
                     lhsT_scale=w1_sc[:, cols],
                     rhs=codes.bitcast(FP8X4),
                     rhs_scale=scales,
-                    start=(a == 0),
-                    stop=(a == 1),
+                    start=(g == 0),
+                    stop=(g == PASSES - 1),
                 )
 
-        a_sb = [sbuf([P, T], F32, "a%d" % t, ("woven1_3", "tab1", "plane2", "plane3")[t]) for t in range(PACK)]
+        a_tags = ("woven1_2", "tab1", "plane2", "plane3")
+        a_sb = [sbuf([P, T], F32, "a%d" % t, a_tags[t]) for t in range(PACK)]
 
         def project_page(t, c):
             acc = next_bank()
-            h, cols = c // 2, slice((c % 2) * BANK, (c % 2 + 1) * BANK)
+            h, part = divmod(c, 2)
+            cols = slice(part * BANK, (part + 1) * BANK)
             project(acc, t, [(page0_codes[h][:, cols], page0_sc[h][:, cols]), (page1_codes[c][:], page1_sc[c][:])])
-            return acc
+            nc.scalar.activation(a_sb[t][:, c * BANK : (c + 1) * BANK], acc[:], ACT.Copy)
 
-        def store_a(t, c, acc, on_vector=False):
-            if on_vector:
-                nc.vector.tensor_copy(a_sb[t][:, c * BANK : (c + 1) * BANK], acc[:])
-            else:
-                nc.scalar.activation(a_sb[t][:, c * BANK : (c + 1) * BANK], acc[:], ACT.Copy)
-
-        dist = [sbuf([P, PACK, BANK], F32, "dist%d" % h, "pairs%d" % h) for h in range(2)]
+        diff = [sbuf([P, PACK, BANK], F32, "dist%d" % h, "pairs%d" % h) for h in range(2)]
+        rate_tags = ("page1_codes3", "woven1_0")
+        rate = [sbuf([P, PACK, BANK], F32, "rate%d" % h, rate_tags[h]) for h in range(2)]
 
         def gather_a(t, h):
-            half = slice(h * LIST_COLS // 2, (h + 1) * LIST_COLS // 2)
             picked = sb.tile([P, BANK], F32, name="picked", tag="picked", bufs=2, align_bytes=64)
-            nc.vector.tensor_copy(picked[:], a_sb[t][:].indirect(pair_list[:, half]))
+            nc.vector.tensor_copy(picked[:], a_sb[t][:].indirect(list_half(pair_list, h)))
             return picked
 
         def subtract_b(t, h, picked):
             acc = next_bank()
             cols = slice(h * BANK, (h + 1) * BANK)
-            project(acc, t, [(v_words[a][:, cols], v_sc[4 * a :, cols]) for a in range(2)])
-            nc.vector.tensor_tensor(dist[h][:, t, :], picked[:], acc[:], ALU.subtract)
+            project(acc, t, [(v_words[g][:, cols], v_sc[4 * g :, cols]) for g in range(PASSES)])
+            nc.vector.tensor_tensor(diff[h][:, t, :], picked[:], acc[:], ALU.subtract)
 
-        rate = [sbuf([P, PACK, BANK], F32, "rate%d" % h, ("page1_codes3", "woven1_0")[h]) for h in range(2)]
+        def compare(first, second):
+            picked = [gather_a(*first), gather_a(*second)]
+            subtract_b(*first, picked[0])
+            subtract_b(*second, picked[1])
 
-        def scale_distance(t, h):
-            nc.scalar.activation(rate[h][:, t, :], dist[h][:, t, :], ACT.Abs, scale=decay_sb[:, t : t + 1])
+        def scale_distances(h):
+            for t in range(PACK):
+                nc.scalar.activation(rate[h][:, t, :], diff[h][:, t, :], ACT.Abs, scale=decay_sb[:, t : t + 1])
 
         def similarity(n, j0, width, tag):
             h, c0 = divmod(j0, BANK)
             sim = sbuf([P, width, PACK], F32, "sim%d" % n, tag)
             nc.scalar.activation(
-                sim[:].rearrange("p (c i) t -> p c t i", i=4),
-                rate[h][:, :, c0 : c0 + width].rearrange("p t (c i) -> p c t i", i=4),
+                sim[:].rearrange("p (c e) t -> p c t e", e=LINE),
+                rate[h][:, :, c0 : c0 + width].rearrange("p t (c e) -> p c t e", e=LINE),
                 ACT.Exp,
                 scale=-1.0,
             )
@@ -261,11 +267,12 @@ def tile_list_mine_loop_closure_kernel(
             nc.vector.tensor_tensor(z[:], sim[:], gain_sb[:].unsqueeze(1).to_broadcast([P, width, PACK]), ALU.mult)
             return z
 
-        def votes(n, z, j0, width):
-            codes = sbuf([P, width], U32, "z_codes%d" % n, "woven1_0" if n == 1 else None)
+        def product_with_w4(n, z, width, codes_tag):
+            codes = sbuf([P, width], U32, "z_codes%d" % n, codes_tag)
             scales = sbuf([P, width], U8, "z_sc%d" % n)
             nc.vector.quantize_mx(out=codes[:].bitcast(FP8X4), scales=scales[:], in_=z[:].rearrange("p c t -> p (c t)"))
-            for u in range(2):
+
+            def rows(u):
                 acc = next_bank()
                 nc.tensor.matmul_mx(
                     out=acc[:, :width],
@@ -276,38 +283,47 @@ def tile_list_mine_loop_closure_kernel(
                     start=True,
                     stop=True,
                 )
-                res = sbuf([P, width], F32, "res%d_%d" % (n, u), "plane%d" % (4 + u) if n == 0 else None)
-                if u == 1 and n == 2:
-                    nc.vector.tensor_scalar(res[:], acc[:, :width], bias_sb[:, u : u + 1], None, ALU.add)
-                else:
-                    nc.scalar.activation(res[:], acc[:, :width], ACT.Identity, bias=bias_sb[:, u : u + 1])
-                (nc.scalar if (u == 0 and n == 2) else nc.sync).dma_start(out[u * P : (u + 1) * P, j0 : j0 + width], res[:])
+                return acc[:, :width]
 
-        def compare(first, second):
-            picked = [gather_a(*first), gather_a(*second)]
-            subtract_b(*first, picked[0])
-            subtract_b(*second, picked[1])
+            return rows
 
-        for t in range(2):
-            for c in range(4):
-                store_a(t, c, project_page(t, c))
+        def store_by_scalar(acc, res, u, j0, queue):
+            nc.scalar.activation(res[:], acc, ACT.Identity, bias=bias_sb[:, u : u + 1])
+            queue.dma_start(out[u * P : (u + 1) * P, j0 : j0 + res.shape[1]], res[:])
+
+        for t in (0, 1):
+            for c in range(CHUNKS):
+                project_page(t, c)
         compare((0, 0), (0, 1))
-        for c in range(4):
+        for c in range(CHUNKS):
             for t in (2, 3):
-                store_a(t, c, project_page(t, c))
+                project_page(t, c)
         compare((1, 0), (1, 1))
         compare((2, 0), (3, 0))
         compare((2, 1), (3, 1))
-        for t in range(4):
-            scale_distance(t, 0)
+
+        quarter = BANK // 2
+        j1, j2 = BANK, BANK + quarter
+        scale_distances(0)
         sim0 = similarity(0, 0, BANK, "w1_raw0")
-        for t in range(4):
-            scale_distance(t, 1)
-        sim1 = similarity(1, BANK, BANK // 2, "w1_raw1")
-        sim2 = similarity(2, BANK + BANK // 2, BANK // 2, "new0")
+        scale_distances(1)
+        sim1 = similarity(1, j1, quarter, "w1_raw1")
+        sim2 = similarity(2, j2, quarter, "new0")
         z0 = weigh(0, sim0, BANK, "plane3")
-        z1 = weigh(1, sim1, BANK // 2, "new2")
-        votes(0, z0, 0, BANK)
-        z2 = weigh(2, sim2, BANK // 2, "new1")
-        votes(1, z1, BANK, BANK // 2)
-        votes(2, z2, BANK + BANK // 2, BANK // 2)
+        z1 = weigh(1, sim1, quarter, "new2")
+        votes0 = product_with_w4(0, z0, BANK, "z_codes0")
+        for u in range(N // P):
+            acc = votes0(u)
+            store_by_scalar(acc, sbuf([P, BANK], F32, "res0_%d" % u, "plane%d" % (PACK + u)), u, 0, nc.sync)
+        z2 = weigh(2, sim2, quarter, "new1")
+        votes1 = product_with_w4(1, z1, quarter, rate_tags[1])
+        for u in range(N // P):
+            acc = votes1(u)
+            store_by_scalar(acc, sbuf([P, quarter], F32, "res1_%d" % u), u, j1, nc.sync)
+        votes2 = product_with_w4(2, z2, quarter, "z_codes2")
+        acc = votes2(0)
+        store_by_scalar(acc, sbuf([P, quarter], F32, "res2_0"), 0, j2, nc.scalar)
+        acc = votes2(1)
+        res = sbuf([P, quarter], F32, "res2_1")
+        nc.vector.tensor_scalar(res[:], acc, bias_sb[:, 1:2], None, ALU.add)
+        nc.sync.dma_start(out[P : 2 * P, j2 : j2 + quarter], res[:])

@@ -166,7 +166,7 @@ def tile_list_mine_loop_closure_kernel(
             scatter(n)
             round_into_words(n)
 
-        page0_codes, page0_sc, page1_codes, page1_sc, v_words = [], [], [], [], []
+        page0_codes, page0_sc, page1_codes, page1_sc = [], [], [], []
 
         def quantise_pass0(h, tag):
             codes = sbuf([P, PAGE_HALF], U32, "page0_codes%d" % h, tag)
@@ -184,12 +184,13 @@ def tile_list_mine_loop_closure_kernel(
             page1_codes.append(codes)
             page1_sc.append(scales)
 
-        def gather_words(g, tag):
-            words = sbuf([P, S], U32, "v_words%d" % g, tag)
-            nc.vector.tensor_copy(words[:], tab[g][:].bitcast(U32).indirect(tab_list[:]))
-            v_words.append(words)
+        def gather_words(g, entries, name, tag):
+            words = sbuf([P, len(entries)], U32, name, tag)
+            offsets = tab_list[:, entries.start // 16 : entries.stop // 16]
+            nc.vector.tensor_copy(words[:], tab[g][:].bitcast(U32).indirect(offsets))
+            return words
 
-        gather_words(0, "v_words0")
+        v0 = [gather_words(0, range(0, BANK), "v0_first", "v0_first")]
         quantise_pass0(0, "new7")
         quantise_pass1(0)
         w1_codes = sbuf([P, PASSES * H], U32, "w1_codes", "woven0_0")
@@ -201,7 +202,8 @@ def tile_list_mine_loop_closure_kernel(
         quantise_pass0(1, "woven1_0")
         quantise_pass1(2)
         quantise_pass1(3)
-        gather_words(1, "woven1_1")
+        v1 = gather_words(1, range(0, S), "v1", "woven1_2")
+        v0.append(gather_words(0, range(BANK, S), "v0_second", "woven1_3"))
 
         def project(acc, t, moving):
             for g in range(PASSES):
@@ -217,7 +219,7 @@ def tile_list_mine_loop_closure_kernel(
                     stop=(g == PASSES - 1),
                 )
 
-        a_tags = ("woven1_2", "tab1", "plane2", "plane3")
+        a_tags = ("plane0", "plane1", "plane2", "plane3")
         a_sb = [sbuf([P, T], F32, "a%d" % t, a_tags[t]) for t in range(PACK)]
 
         def project_page(t, c):
@@ -228,8 +230,8 @@ def tile_list_mine_loop_closure_kernel(
             nc.scalar.activation(a_sb[t][:, c * BANK : (c + 1) * BANK], acc[:], ACT.Copy)
 
         diff = [sbuf([P, PACK, BANK], F32, "dist%d" % h, "pairs%d" % h) for h in range(2)]
-        rate_tags = ("page1_codes3", "woven1_0")
-        rate = [sbuf([P, PACK, BANK], F32, "rate%d" % h, rate_tags[h]) for h in range(2)]
+        rate_parts = ((0, BANK, "page1_codes3"), (BANK, BANK - P, "woven1_0"), (S - P, P, "rate2"))
+        rate = [sbuf([P, PACK, width], F32, "rate%d" % n, tag) for n, (j0, width, tag) in enumerate(rate_parts)]
 
         def gather_a(t, h):
             picked = sb.tile([P, BANK], F32, name="picked", tag="picked", bufs=2, align_bytes=64)
@@ -239,7 +241,7 @@ def tile_list_mine_loop_closure_kernel(
         def subtract_b(t, h, picked):
             acc = next_bank()
             cols = slice(h * BANK, (h + 1) * BANK)
-            project(acc, t, [(v_words[g][:, cols], v_sc[4 * g :, cols]) for g in range(PASSES)])
+            project(acc, t, [(v0[h][:], v_sc[:, cols]), (v1[:, cols], v_sc[4:, cols])])
             nc.vector.tensor_tensor(diff[h][:, t, :], picked[:], acc[:], ALU.subtract)
 
         def compare(first, second):
@@ -247,35 +249,46 @@ def tile_list_mine_loop_closure_kernel(
             subtract_b(*first, picked[0])
             subtract_b(*second, picked[1])
 
-        def scale_distances(h):
-            for t in range(PACK):
-                nc.scalar.activation(rate[h][:, t, :], diff[h][:, t, :], ACT.Abs, scale=decay_sb[:, t : t + 1])
+        def fetch_b(t, h, tag):
+            acc = next_bank()
+            cols = slice(h * BANK, (h + 1) * BANK)
+            project(acc, t, [(v0[h][:], v_sc[:, cols]), (v1[:, cols], v_sc[4:, cols])])
+            b_sb = sbuf([P, BANK], F32, "b%d_%d" % (t, h), tag)
+            nc.scalar.activation(b_sb[:], acc[:], ACT.Copy)
+            return b_sb
 
-        def similarity(n, j0, width, tag):
-            h, c0 = divmod(j0, BANK)
+        def gather_minus_b(t, h, b_sb):
+            nc.vector.tensor_tensor(diff[h][:, t, :], a_sb[t][:].indirect(list_half(pair_list, h)), b_sb[:], ALU.subtract)
+
+        def scale_distance(t, h):
+            for part, (j0, width, tag) in zip(rate, rate_parts):
+                if j0 // BANK == h:
+                    c0 = j0 % BANK
+                    nc.scalar.activation(part[:, t, :], diff[h][:, t, c0 : c0 + width], ACT.Abs, scale=decay_sb[:, t : t + 1])
+
+        def similarity(n, part, c0, width, tag):
             sim = sbuf([P, width, PACK], F32, "sim%d" % n, tag)
             nc.scalar.activation(
                 sim[:].rearrange("p (c e) t -> p c t e", e=LINE),
-                rate[h][:, :, c0 : c0 + width].rearrange("p t (c e) -> p c t e", e=LINE),
+                rate[part][:, :, c0 : c0 + width].rearrange("p t (c e) -> p c t e", e=LINE),
                 ACT.Exp,
                 scale=-1.0,
             )
             return sim
 
-        def weigh(n, sim, width, tag):
-            z = sbuf([P, width, PACK], BF16, "z%d" % n, tag)
-            nc.vector.tensor_tensor(z[:], sim[:], gain_sb[:].unsqueeze(1).to_broadcast([P, width, PACK]), ALU.mult)
-            return z
+        def weigh(z, sim):
+            nc.vector.tensor_tensor(z, sim[:], gain_sb[:].unsqueeze(1).to_broadcast(list(z.shape)), ALU.mult)
 
         def product_with_w4(n, z, width, codes_tag):
             codes = sbuf([P, width], U32, "z_codes%d" % n, codes_tag)
             scales = sbuf([P, width], U8, "z_sc%d" % n)
             nc.vector.quantize_mx(out=codes[:].bitcast(FP8X4), scales=scales[:], in_=z[:].rearrange("p c t -> p (c t)"))
 
-            def rows(u):
-                acc = next_bank()
+            def rows(u, acc=None):
+                if acc is None:
+                    acc = next_bank()[:, :width]
                 nc.tensor.matmul_mx(
-                    out=acc[:, :width],
+                    out=acc,
                     lhsT=w4[:, 2 * P * u : 2 * P * (u + 1)].bitcast(FP4X4),
                     lhsT_scale=w4_sc[:, P * u : P * (u + 1)],
                     rhs=codes[:].bitcast(FP8X4),
@@ -283,7 +296,7 @@ def tile_list_mine_loop_closure_kernel(
                     start=True,
                     stop=True,
                 )
-                return acc[:, :width]
+                return acc
 
             return rows
 
@@ -291,39 +304,57 @@ def tile_list_mine_loop_closure_kernel(
             nc.scalar.activation(res[:], acc, ACT.Identity, bias=bias_sb[:, u : u + 1])
             queue.dma_start(out[u * P : (u + 1) * P, j0 : j0 + res.shape[1]], res[:])
 
-        for t in (0, 1):
+        for t in (0, 1, 2):
             for c in range(CHUNKS):
                 project_page(t, c)
         compare((0, 0), (0, 1))
         for c in range(CHUNKS):
-            for t in (2, 3):
-                project_page(t, c)
+            project_page(3, c)
+        late = [(2, 0), (3, 0), (2, 1), (3, 1)]
+        b_late = [fetch_b(t, h, "new%d" % (3 + t)) for t, h in late[:2]]
+        scale_distance(0, 0)
+        scale_distance(0, 1)
         compare((1, 0), (1, 1))
-        compare((2, 0), (3, 0))
-        compare((2, 1), (3, 1))
+        b_late.extend(fetch_b(t, h, "new%d" % (1 + t)) for t, h in late[2:])
+        scale_distance(1, 0)
+        scale_distance(1, 1)
+        for (t, h), b_sb in zip(late, b_late):
+            gather_minus_b(t, h, b_sb)
 
         quarter = BANK // 2
-        j1, j2 = BANK, BANK + quarter
-        scale_distances(0)
-        sim0 = similarity(0, 0, BANK, "w1_raw0")
-        scale_distances(1)
-        sim1 = similarity(1, j1, quarter, "w1_raw1")
-        sim2 = similarity(2, j2, quarter, "new0")
-        z0 = weigh(0, sim0, BANK, "plane3")
-        z1 = weigh(1, sim1, quarter, "new2")
+        scale_distance(2, 0)
+        scale_distance(3, 0)
+        sim0 = [similarity(0, 0, 0, quarter, "w1_raw0"), similarity(1, 0, quarter, quarter, "w1_raw1")]
+        scale_distance(2, 1)
+        scale_distance(3, 1)
+        sim1 = similarity(2, 1, 0, quarter, "woven0_1")
+        sim2 = similarity(3, 1, quarter, P, "new0")
+        sim3 = similarity(4, 2, 0, P, "sim4")
+        z0 = sbuf([P, BANK, PACK], BF16, "z0", "plane2")
+        for q in range(2):
+            weigh(z0[:, q * quarter : (q + 1) * quarter, :], sim0[q])
         votes0 = product_with_w4(0, z0, BANK, "z_codes0")
+        z1 = sbuf([P, quarter, PACK], BF16, "z1", "new2")
+        weigh(z1[:], sim1)
+        z2 = sbuf([P, P, PACK], BF16, "z2", "new1")
+        weigh(z2[:], sim2)
+        votes1 = product_with_w4(1, z1, quarter, rate_parts[1][2])
+        z3 = sbuf([P, P, PACK], BF16, "z3")
+        weigh(z3[:], sim3)
+        votes2 = product_with_w4(2, z2, P, rate_parts[2][2])
+        votes3 = product_with_w4(3, z3, P, "z_codes3")
         for u in range(N // P):
             acc = votes0(u)
             store_by_scalar(acc, sbuf([P, BANK], F32, "res0_%d" % u, "plane%d" % (PACK + u)), u, 0, nc.sync)
-        z2 = weigh(2, sim2, quarter, "new1")
-        votes1 = product_with_w4(1, z1, quarter, rate_tags[1])
         for u in range(N // P):
             acc = votes1(u)
-            store_by_scalar(acc, sbuf([P, quarter], F32, "res1_%d" % u), u, j1, nc.sync)
-        votes2 = product_with_w4(2, z2, quarter, "z_codes2")
-        acc = votes2(0)
-        store_by_scalar(acc, sbuf([P, quarter], F32, "res2_0"), 0, j2, nc.scalar)
-        acc = votes2(1)
+            store_by_scalar(acc, sbuf([P, quarter], F32, "res1_%d" % u), u, BANK, nc.sync)
+        j_last = BANK + quarter
+        last = [next_bank(), next_bank()]
+        for votes, c0 in ((votes2, 0), (votes3, P)):
+            for u in range(N // P):
+                votes(u, last[u][:, c0 : c0 + P])
+        store_by_scalar(last[0][:, :quarter], sbuf([P, quarter], F32, "res2_0"), 0, j_last, nc.scalar)
         res = sbuf([P, quarter], F32, "res2_1")
-        nc.vector.tensor_scalar(res[:], acc, bias_sb[:, 1:2], None, ALU.add)
-        nc.sync.dma_start(out[P : 2 * P, j2 : j2 + quarter], res[:])
+        nc.vector.tensor_scalar(res[:], last[1][:, :quarter], bias_sb[:, 1:2], None, ALU.add)
+        nc.sync.dma_start(out[P : 2 * P, j_last : j_last + quarter], res[:])

@@ -26,8 +26,8 @@ PSUM_BANKS = 8
 CHUNKS = T // BANK
 PAGE_HALF = T // 2
 LIST_COLS = S // 16
+FIRST_CUTS = (0, S // 4, S)
 LINE = 4
-TAB_TAIL = 128
 
 
 def tile_list_mine_loop_closure_kernel(
@@ -69,37 +69,35 @@ def tile_list_mine_loop_closure_kernel(
 
         planes, news = [], []
 
-        def load_plane(n, pieces):
+        def load_plane(n, cuts):
             g, i = divmod(n, PACK)
             rows = slice(g * K_PASS, (g + 1) * K_PASS)
             plane = sbuf([P, T], F32, "plane%d" % n)
             new = sbuf([P, S], F32, "new%d" % n)
             nc.sync.dma_start(plane[:], base[rows, :].rearrange("(p i) t -> p i t", i=PACK)[:, i, :])
             xs_rows = xs[rows, :].rearrange("(p i) m -> p i m", i=PACK)[:, i, :]
-            for piece in range(pieces):
-                cols = slice(piece * S // pieces, (piece + 1) * S // pieces)
-                nc.sync.dma_start(new[:, cols], xs_rows[:, cols])
+            for first, last in zip(cuts, cuts[1:]):
+                nc.sync.dma_start(new[:, first:last], xs_rows[:, first:last])
             planes.append(plane)
             news.append(new)
 
-        load_plane(0, 2)
-        load_plane(1, 1)
+        load_plane(0, FIRST_CUTS)
+        load_plane(1, (0, S))
         w1_raw = []
         for g in range(PASSES):
             raw = sbuf([P, PACK, H], F32, "w1_raw%d" % g)
             nc.sync.dma_start(raw[:], w1[g * K_PASS : (g + 1) * K_PASS, :].rearrange("(p i) r -> p i r", i=PACK))
             w1_raw.append(raw)
         for n in range(2, 6):
-            load_plane(n, 1)
+            load_plane(n, (0, S))
         tab_hbm = [tab_words[g].rearrange("p t i -> p (t i)").bitcast(I32) for g in range(PASSES)]
         tab = []
-        for g, early_cols in enumerate((T - TAB_TAIL, T)):
+        for g in range(PASSES):
             words = sbuf([P, T], I32, "tab%d" % g)
-            nc.sync.dma_start(words[:, :early_cols], tab_hbm[g][:, :early_cols])
+            nc.sync.dma_start(words[:], tab_hbm[g])
             tab.append(words)
-        load_plane(6, 1)
-        load_plane(7, 1)
-        nc.sync.dma_start(tab[0][:, T - TAB_TAIL :], tab_hbm[0][:, T - TAB_TAIL :])
+        load_plane(6, (0, S))
+        load_plane(7, (0, S))
         nc.sync.dma_start(pair_list[:], offs3)
         decay_sb = sbuf([P, PACK], F32, "decay_sb")
         gain_sb = sbuf([P, PACK], F32, "gain_sb")
@@ -127,12 +125,12 @@ def tile_list_mine_loop_closure_kernel(
 
         woven1 = [sbuf([P, BANK, PACK], BF16, "woven1_%d" % c) for c in range(CHUNKS)]
 
-        def round_into_words(n):
-            for c in range(CHUNKS):
+        def round_into_words(n, chunks):
+            for c in range(chunks):
                 nc.scalar.activation(woven1[c][:, :, n - PACK], planes[n][:, c * BANK : (c + 1) * BANK], ACT.Copy)
 
-        for h in range(2):
-            nc.vector.tensor_copy(planes[0][:].indirect(list_half(slot_list, h)), news[0][:, h * S // 2 : (h + 1) * S // 2])
+        for first, last in zip(FIRST_CUTS, FIRST_CUTS[1:]):
+            nc.vector.tensor_copy(planes[0][:].indirect(slot_list[:, first // 16 : last // 16]), news[0][:, first:last])
         round_into_pairs(0)
         w1_woven = sbuf([P, PASSES, PACK * H], BF16, "w1_bf")
         for g in range(PASSES):
@@ -156,22 +154,35 @@ def tile_list_mine_loop_closure_kernel(
         for n in (4, 5):
             scatter(n)
             round_into_pairs(n)
-        for c in range(CHUNKS):
+        def words_of(c):
+            return woven1[c][:].rearrange("p c i -> p (c i)").bitcast(F32).rearrange("p (c u) -> p c u", u=2)
+
+        for c in range(CHUNKS - 1):
             h, part = divmod(c, 2)
             nc.scalar.copy(
-                woven1[c][:].rearrange("p c i -> p (c i)").bitcast(F32).rearrange("p (c u) -> p c u", u=2),
-                pairs[h][:, 0, part * BANK : (part + 1) * BANK, :].bitcast(F32).to_broadcast([P, BANK, 2]),
+                words_of(c), pairs[h][:, 0, part * BANK : (part + 1) * BANK, :].bitcast(F32).to_broadcast([P, BANK, 2])
             )
-        for n in (6, 7):
-            scatter(n)
-            round_into_words(n)
+        scatter(6)
+        round_into_words(6, 2)
+        nc.scalar.activation(
+            woven1[2][:, :, 2:4], planes[6][:, 2 * BANK : 3 * BANK].unsqueeze(2).to_broadcast([P, BANK, 2]), ACT.Copy
+        )
+        nc.scalar.activation(pairs[1][:, 1, BANK:, 0], planes[6][:, T - BANK :], ACT.Copy)
+        nc.scalar.copy(
+            words_of(CHUNKS - 1),
+            pairs[1][:, :, BANK:, :].rearrange("p u c e -> p u (c e)").bitcast(F32).rearrange("p u c -> p c u"),
+        )
+        scatter(7)
+        round_into_words(7, 2)
 
         page0_codes, page0_sc, page1_codes, page1_sc = [], [], [], []
 
+        held_sc = sbuf([P, 3, PAGE_HALF], U8, "held_sc", "new7")
+
         def quantise_pass0(h, tag):
             codes = sbuf([P, PAGE_HALF], U32, "page0_codes%d" % h, tag)
-            scales = sbuf([P, PAGE_HALF], U8, "page0_sc%d" % h)
-            nc.vector.quantize_mx(out=codes[:].bitcast(FP8X4), scales=scales[:], in_=woven0[h][:])
+            scales = held_sc[:, h, :]
+            nc.vector.quantize_mx(out=codes[:].bitcast(FP8X4), scales=scales, in_=woven0[h][:])
             page0_codes.append(codes)
             page0_sc.append(scales)
 
@@ -190,20 +201,24 @@ def tile_list_mine_loop_closure_kernel(
             nc.vector.tensor_copy(words[:], tab[g][:].bitcast(U32).indirect(offsets))
             return words
 
-        v0 = [gather_words(0, range(0, BANK), "v0_first", "v0_first")]
-        quantise_pass0(0, "new7")
-        quantise_pass1(0)
-        w1_codes = sbuf([P, PASSES * H], U32, "w1_codes", "woven0_0")
-        w1_sc = sbuf([P, PASSES * H], U8, "w1_sc")
+        w1_codes = sbuf([P, PASSES * H], U32, "w1_codes", "new6")
+        w1_sc = held_sc[:, 2, :]
         nc.vector.quantize_mx(
-            out=w1_codes[:].bitcast(FP8X4), scales=w1_sc[:], in_=w1_woven[:].rearrange("p g c -> p (g c)")
+            out=w1_codes[:].bitcast(FP8X4), scales=w1_sc, in_=w1_woven[:].rearrange("p g c -> p (g c)")
         )
+        quantise_pass0(0, "page0_codes0")
+        quantise_pass1(0)
+        nc.vector.tensor_copy(woven1[2][:, :, 3], planes[7][:, 2 * BANK : 3 * BANK])
         quantise_pass1(1)
-        quantise_pass0(1, "woven1_0")
+        nc.vector.tensor_copy(woven1[3][:, :, 3], planes[7][:, 3 * BANK : 4 * BANK])
+        quantise_pass0(1, "page0_codes1")
         quantise_pass1(2)
         quantise_pass1(3)
-        v1 = gather_words(1, range(0, S), "v1", "woven1_2")
-        v0.append(gather_words(0, range(BANK, S), "v0_second", "woven1_3"))
+        word_tags = {(0, 0): "woven1_1", (1, 0): "woven1_2", (0, 1): "woven1_3", (1, 1): "woven0_1"}
+        v_words = {}
+        for h in range(2):
+            for g in range(PASSES):
+                v_words[g, h] = gather_words(g, range(h * BANK, (h + 1) * BANK), "v%d_%d" % (g, h), word_tags[g, h])
 
         def project(acc, t, moving):
             for g in range(PASSES):
@@ -230,29 +245,18 @@ def tile_list_mine_loop_closure_kernel(
             nc.scalar.activation(a_sb[t][:, c * BANK : (c + 1) * BANK], acc[:], ACT.Copy)
 
         diff = [sbuf([P, PACK, BANK], F32, "dist%d" % h, "pairs%d" % h) for h in range(2)]
-        rate_parts = ((0, BANK, "page1_codes3"), (BANK, BANK - P, "woven1_0"), (S - P, P, "rate2"))
+        rate_parts = (
+            (0, BANK, "page1_codes3"),
+            (BANK, 2 * P, "page0_codes1"),
+            (S - 2 * P, P, "rate2"),
+            (S - P, P, "rate3"),
+        )
         rate = [sbuf([P, PACK, width], F32, "rate%d" % n, tag) for n, (j0, width, tag) in enumerate(rate_parts)]
-
-        def gather_a(t, h):
-            picked = sb.tile([P, BANK], F32, name="picked", tag="picked", bufs=2, align_bytes=64)
-            nc.vector.tensor_copy(picked[:], a_sb[t][:].indirect(list_half(pair_list, h)))
-            return picked
-
-        def subtract_b(t, h, picked):
-            acc = next_bank()
-            cols = slice(h * BANK, (h + 1) * BANK)
-            project(acc, t, [(v0[h][:], v_sc[:, cols]), (v1[:, cols], v_sc[4:, cols])])
-            nc.vector.tensor_tensor(diff[h][:, t, :], picked[:], acc[:], ALU.subtract)
-
-        def compare(first, second):
-            picked = [gather_a(*first), gather_a(*second)]
-            subtract_b(*first, picked[0])
-            subtract_b(*second, picked[1])
 
         def fetch_b(t, h, tag):
             acc = next_bank()
             cols = slice(h * BANK, (h + 1) * BANK)
-            project(acc, t, [(v0[h][:], v_sc[:, cols]), (v1[:, cols], v_sc[4:, cols])])
+            project(acc, t, [(v_words[g, h][:], v_sc[4 * g :, cols]) for g in range(PASSES)])
             b_sb = sbuf([P, BANK], F32, "b%d_%d" % (t, h), tag)
             nc.scalar.activation(b_sb[:], acc[:], ACT.Copy)
             return b_sb
@@ -260,11 +264,13 @@ def tile_list_mine_loop_closure_kernel(
         def gather_minus_b(t, h, b_sb):
             nc.vector.tensor_tensor(diff[h][:, t, :], a_sb[t][:].indirect(list_half(pair_list, h)), b_sb[:], ALU.subtract)
 
-        def scale_distance(t, h):
-            for part, (j0, width, tag) in zip(rate, rate_parts):
-                if j0 // BANK == h:
-                    c0 = j0 % BANK
-                    nc.scalar.activation(part[:, t, :], diff[h][:, t, c0 : c0 + width], ACT.Abs, scale=decay_sb[:, t : t + 1])
+        def scale_distances(part):
+            j0, width, tag = rate_parts[part]
+            h, c0 = divmod(j0, BANK)
+            for t in range(PACK):
+                nc.scalar.activation(
+                    rate[part][:, t, :], diff[h][:, t, c0 : c0 + width], ACT.Abs, scale=decay_sb[:, t : t + 1]
+                )
 
         def similarity(n, part, c0, width, tag):
             sim = sbuf([P, width, PACK], F32, "sim%d" % n, tag)
@@ -304,48 +310,47 @@ def tile_list_mine_loop_closure_kernel(
             nc.scalar.activation(res[:], acc, ACT.Identity, bias=bias_sb[:, u : u + 1])
             queue.dma_start(out[u * P : (u + 1) * P, j0 : j0 + res.shape[1]], res[:])
 
-        for t in (0, 1, 2):
-            for c in range(CHUNKS):
+        for c in (0, 1):
+            for t in range(PACK):
                 project_page(t, c)
-        compare((0, 0), (0, 1))
-        for c in range(CHUNKS):
-            project_page(3, c)
-        late = [(2, 0), (3, 0), (2, 1), (3, 1)]
-        b_late = [fetch_b(t, h, "new%d" % (3 + t)) for t, h in late[:2]]
-        scale_distance(0, 0)
-        scale_distance(0, 1)
-        compare((1, 0), (1, 1))
-        b_late.extend(fetch_b(t, h, "new%d" % (1 + t)) for t, h in late[2:])
-        scale_distance(1, 0)
-        scale_distance(1, 1)
-        for (t, h), b_sb in zip(late, b_late):
-            gather_minus_b(t, h, b_sb)
+        b_sb = {}
+        for tiles in ((0, 1), (2,), (3,)):
+            for t in tiles:
+                for c in (2, 3):
+                    project_page(t, c)
+            for t in tiles:
+                b_sb[t, 0] = fetch_b(t, 0, "b%d" % t)
+        for t in range(PACK):
+            b_sb[t, 1] = fetch_b(t, 1, "new%d" % (2 + t))
+        for h in range(2):
+            for t in range(PACK):
+                gather_minus_b(t, h, b_sb[t, h])
 
         quarter = BANK // 2
-        scale_distance(2, 0)
-        scale_distance(3, 0)
+        scale_distances(0)
         sim0 = [similarity(0, 0, 0, quarter, "w1_raw0"), similarity(1, 0, quarter, quarter, "w1_raw1")]
-        scale_distance(2, 1)
-        scale_distance(3, 1)
-        sim1 = similarity(2, 1, 0, quarter, "woven0_1")
-        sim2 = similarity(3, 1, quarter, P, "new0")
-        sim3 = similarity(4, 2, 0, P, "sim4")
+        scale_distances(1)
+        sim1 = similarity(2, 1, 0, quarter, "woven0_0")
+        scale_distances(2)
+        scale_distances(3)
+        sim2 = similarity(3, 2, 0, P, "new0")
+        sim3 = similarity(4, 3, 0, P, "sim4")
         z0 = sbuf([P, BANK, PACK], BF16, "z0", "plane2")
         for q in range(2):
             weigh(z0[:, q * quarter : (q + 1) * quarter, :], sim0[q])
         votes0 = product_with_w4(0, z0, BANK, "z_codes0")
-        z1 = sbuf([P, quarter, PACK], BF16, "z1", "new2")
+        z1 = sbuf([P, quarter, PACK], BF16, "z1", "b0")
         weigh(z1[:], sim1)
         z2 = sbuf([P, P, PACK], BF16, "z2", "new1")
         weigh(z2[:], sim2)
-        votes1 = product_with_w4(1, z1, quarter, rate_parts[1][2])
+        votes1 = product_with_w4(1, z1, quarter, rate_parts[2][2])
         z3 = sbuf([P, P, PACK], BF16, "z3")
         weigh(z3[:], sim3)
-        votes2 = product_with_w4(2, z2, P, rate_parts[2][2])
+        votes2 = product_with_w4(2, z2, P, rate_parts[3][2])
         votes3 = product_with_w4(3, z3, P, "z_codes3")
         for u in range(N // P):
             acc = votes0(u)
-            store_by_scalar(acc, sbuf([P, BANK], F32, "res0_%d" % u, "plane%d" % (PACK + u)), u, 0, nc.sync)
+            store_by_scalar(acc, sbuf([P, BANK], F32, "res0_%d" % u, ("woven0_0", "new0")[u]), u, 0, nc.sync)
         for u in range(N // P):
             acc = votes1(u)
             store_by_scalar(acc, sbuf([P, quarter], F32, "res1_%d" % u), u, BANK, nc.sync)

@@ -26,8 +26,7 @@ PSUM_BANKS = 8
 CHUNKS = T // BANK
 PAGE_HALF = T // 2
 LIST_COLS = S // 16
-FIRST_CUTS = (0, S // 4, S)
-LINE = 4
+FIRST_CUT = S // 4
 
 
 def tile_list_mine_loop_closure_kernel(
@@ -57,8 +56,15 @@ def tile_list_mine_loop_closure_kernel(
         tab_sc = sbuf([P, T], U8, "tab_sc")
         nc.vector.memset(tab_sc[:].bitcast(I32), 0)
         w4_sc = sbuf([P, N], U8, "w4_sc")
-        nc.vector.memset(w4_sc[:].bitcast(I32), 0)
+        nc.gpsimd.memset(w4_sc[:].bitcast(I32), 0)
         nc.sync.dma_start(tab_list[:], offs)
+        news = [sbuf([P, S], F32, "new%d" % n) for n in range(PASSES * PACK)]
+
+        def load_new(n, first, last):
+            g, i = divmod(n, PACK)
+            xs_rows = xs[g * K_PASS : (g + 1) * K_PASS, :].rearrange("(p i) m -> p i m", i=PACK)[:, i, :]
+            nc.sync.dma_start(news[n][:, first:last], xs_rows[:, first:last])
+
         for q in range(QUADRANTS):
             nc.sync.dma_start(
                 tab_sc[32 * q : 32 * q + 4 * PASSES, :].bitcast(I32), tab_scales[:, 4 * q : 4 * q + 4, :].bitcast(I32)
@@ -67,37 +73,34 @@ def tile_list_mine_loop_closure_kernel(
         v_sc = sbuf([P, S], U8, "v_sc")
         nc.vector.tensor_copy(v_sc[:], tab_sc[:].indirect(tab_list[:]))
 
-        planes, news = [], []
+        planes = []
 
-        def load_plane(n, cuts):
+        def load_plane(n, first_new):
             g, i = divmod(n, PACK)
-            rows = slice(g * K_PASS, (g + 1) * K_PASS)
             plane = sbuf([P, T], F32, "plane%d" % n)
-            new = sbuf([P, S], F32, "new%d" % n)
-            nc.sync.dma_start(plane[:], base[rows, :].rearrange("(p i) t -> p i t", i=PACK)[:, i, :])
-            xs_rows = xs[rows, :].rearrange("(p i) m -> p i m", i=PACK)[:, i, :]
-            for first, last in zip(cuts, cuts[1:]):
-                nc.sync.dma_start(new[:, first:last], xs_rows[:, first:last])
+            nc.sync.dma_start(plane[:], base[g * K_PASS : (g + 1) * K_PASS, :].rearrange("(p i) t -> p i t", i=PACK)[:, i, :])
+            if first_new:
+                load_new(n, 0, first_new)
+            load_new(n, first_new, S)
             planes.append(plane)
-            news.append(new)
 
-        load_plane(0, FIRST_CUTS)
-        load_plane(1, (0, S))
+        load_plane(0, FIRST_CUT)
+        load_plane(1, 0)
         w1_raw = []
         for g in range(PASSES):
             raw = sbuf([P, PACK, H], F32, "w1_raw%d" % g)
             nc.sync.dma_start(raw[:], w1[g * K_PASS : (g + 1) * K_PASS, :].rearrange("(p i) r -> p i r", i=PACK))
             w1_raw.append(raw)
         for n in range(2, 6):
-            load_plane(n, (0, S))
+            load_plane(n, 0)
         tab_hbm = [tab_words[g].rearrange("p t i -> p (t i)").bitcast(I32) for g in range(PASSES)]
         tab = []
         for g in range(PASSES):
             words = sbuf([P, T], I32, "tab%d" % g)
             nc.sync.dma_start(words[:], tab_hbm[g])
             tab.append(words)
-        load_plane(6, (0, S))
-        load_plane(7, (0, S))
+        load_plane(6, 0)
+        load_plane(7, 0)
         nc.sync.dma_start(pair_list[:], offs3)
         decay_sb = sbuf([P, PACK], F32, "decay_sb")
         gain_sb = sbuf([P, PACK], F32, "gain_sb")
@@ -129,7 +132,7 @@ def tile_list_mine_loop_closure_kernel(
             for c in range(chunks):
                 nc.scalar.activation(woven1[c][:, :, n - PACK], planes[n][:, c * BANK : (c + 1) * BANK], ACT.Copy)
 
-        for first, last in zip(FIRST_CUTS, FIRST_CUTS[1:]):
+        for first, last in ((0, FIRST_CUT), (FIRST_CUT, S)):
             nc.vector.tensor_copy(planes[0][:].indirect(slot_list[:, first // 16 : last // 16]), news[0][:, first:last])
         round_into_pairs(0)
         w1_woven = sbuf([P, PASSES, PACK * H], BF16, "w1_bf")
@@ -175,16 +178,19 @@ def tile_list_mine_loop_closure_kernel(
         scatter(7)
         round_into_words(7, 2)
 
-        page0_codes, page0_sc, page1_codes, page1_sc = [], [], [], []
+        page1_codes, page1_sc = {}, {}
 
         held_sc = sbuf([P, 3, PAGE_HALF], U8, "held_sc", "new7")
 
-        def quantise_pass0(h, tag):
-            codes = sbuf([P, PAGE_HALF], U32, "page0_codes%d" % h, tag)
-            scales = held_sc[:, h, :]
-            nc.vector.quantize_mx(out=codes[:].bitcast(FP8X4), scales=scales, in_=woven0[h][:])
-            page0_codes.append(codes)
-            page0_sc.append(scales)
+        page0_codes = [sbuf([P, PAGE_HALF], U32, "page0_codes%d" % h) for h in range(2)]
+        page0_sc = [held_sc[:, h, :] for h in range(2)]
+
+        def quantise_pass0(h, first, last):
+            nc.vector.quantize_mx(
+                out=page0_codes[h][:, first:last].bitcast(FP8X4),
+                scales=page0_sc[h][:, first:last],
+                in_=woven0[h][:, PACK * first : PACK * last],
+            )
 
         def quantise_pass1(c):
             codes = sbuf([P, BANK], U32, "page1_codes%d" % c)
@@ -192,8 +198,7 @@ def tile_list_mine_loop_closure_kernel(
             nc.vector.quantize_mx(
                 out=codes[:].bitcast(FP8X4), scales=scales[:], in_=woven1[c][:].rearrange("p c i -> p (c i)")
             )
-            page1_codes.append(codes)
-            page1_sc.append(scales)
+            page1_codes[c], page1_sc[c] = codes, scales
 
         def gather_words(g, entries, name, tag):
             words = sbuf([P, len(entries)], U32, name, tag)
@@ -203,18 +208,23 @@ def tile_list_mine_loop_closure_kernel(
 
         w1_codes = sbuf([P, PASSES * H], U32, "w1_codes", "new6")
         w1_sc = held_sc[:, 2, :]
-        nc.vector.quantize_mx(
-            out=w1_codes[:].bitcast(FP8X4), scales=w1_sc, in_=w1_woven[:].rearrange("p g c -> p (g c)")
-        )
-        quantise_pass0(0, "page0_codes0")
+
+        def quantise_w1(g):
+            cols = slice(g * H, (g + 1) * H)
+            nc.vector.quantize_mx(out=w1_codes[:, cols].bitcast(FP8X4), scales=w1_sc[:, cols], in_=w1_woven[:, g, :])
+
+        quantise_w1(0)
+        quantise_pass0(0, 0, BANK)
+        quantise_w1(1)
+        nc.vector.tensor_copy(woven1[3][:, :, 3], planes[7][:, 3 * BANK : 4 * BANK])
         quantise_pass1(0)
+        quantise_pass0(0, BANK, 2 * BANK)
         nc.vector.tensor_copy(woven1[2][:, :, 3], planes[7][:, 2 * BANK : 3 * BANK])
         quantise_pass1(1)
-        nc.vector.tensor_copy(woven1[3][:, :, 3], planes[7][:, 3 * BANK : 4 * BANK])
-        quantise_pass0(1, "page0_codes1")
-        quantise_pass1(2)
+        quantise_pass0(1, 0, 2 * BANK)
         quantise_pass1(3)
-        word_tags = {(0, 0): "woven1_1", (1, 0): "woven1_2", (0, 1): "woven1_3", (1, 1): "woven0_1"}
+        quantise_pass1(2)
+        word_tags = {(0, 0): "woven1_1", (1, 0): "woven1_3", (0, 1): "woven1_2", (1, 1): "woven0_1"}
         v_words = {}
         for h in range(2):
             for g in range(PASSES):
@@ -246,7 +256,7 @@ def tile_list_mine_loop_closure_kernel(
 
         diff = [sbuf([P, PACK, BANK], F32, "dist%d" % h, "pairs%d" % h) for h in range(2)]
         rate_parts = (
-            (0, BANK, "page1_codes3"),
+            (0, BANK, "page1_codes2"),
             (BANK, 2 * P, "page0_codes1"),
             (S - 2 * P, P, "rate2"),
             (S - P, P, "rate3"),
@@ -273,17 +283,18 @@ def tile_list_mine_loop_closure_kernel(
                 )
 
         def similarity(n, part, c0, width, tag):
-            sim = sbuf([P, width, PACK], F32, "sim%d" % n, tag)
-            nc.scalar.activation(
-                sim[:].rearrange("p (c e) t -> p c t e", e=LINE),
-                rate[part][:, :, c0 : c0 + width].rearrange("p t (c e) -> p c t e", e=LINE),
-                ACT.Exp,
-                scale=-1.0,
-            )
+            sim = sbuf([P, PACK, width], F32, "sim%d" % n, tag)
+            nc.scalar.activation(sim[:], rate[part][:, :, c0 : c0 + width], ACT.Exp, scale=-1.0)
             return sim
 
         def weigh(z, sim):
-            nc.vector.tensor_tensor(z, sim[:], gain_sb[:].unsqueeze(1).to_broadcast(list(z.shape)), ALU.mult)
+            width = z.shape[1]
+            nc.vector.tensor_tensor(
+                z.rearrange("p (c e) t -> p c t e", e=2),
+                sim[:].rearrange("p t (c e) -> p c t e", e=2),
+                gain_sb[:].unsqueeze(1).unsqueeze(3).to_broadcast([P, width // 2, PACK, 2]),
+                ALU.mult,
+            )
 
         def product_with_w4(n, z, width, codes_tag):
             codes = sbuf([P, width], U32, "z_codes%d" % n, codes_tag)
@@ -316,7 +327,7 @@ def tile_list_mine_loop_closure_kernel(
         b_sb = {}
         for tiles in ((0, 1), (2,), (3,)):
             for t in tiles:
-                for c in (2, 3):
+                for c in (3, 2):
                     project_page(t, c)
             for t in tiles:
                 b_sb[t, 0] = fetch_b(t, 0, "b%d" % t)

@@ -26,6 +26,7 @@ PSUM_BANKS = 8
 CHUNKS = T // BANK
 PAGE_HALF = T // 2
 LIST_COLS = S // 16
+SHARED_CUT = BANK // 2
 FIRST_CUT = S // 4
 
 
@@ -167,8 +168,13 @@ def tile_list_mine_loop_closure_kernel(
             )
         scatter(6)
         round_into_words(6, 2)
-        nc.scalar.activation(
-            woven1[2][:, :, 2:4], planes[6][:, 2 * BANK : 3 * BANK].unsqueeze(2).to_broadcast([P, BANK, 2]), ACT.Copy
+        nc.gpsimd.tensor_scalar(
+            woven1[2][:, :, 2:4],
+            planes[6][:, 2 * BANK : 3 * BANK].unsqueeze(2).to_broadcast([P, BANK, 2]),
+            1.0,
+            0.0,
+            ALU.mult,
+            ALU.add,
         )
         nc.scalar.activation(pairs[1][:, 1, BANK:, 0], planes[6][:, T - BANK :], ACT.Copy)
         nc.scalar.copy(
@@ -177,6 +183,7 @@ def tile_list_mine_loop_closure_kernel(
         )
         scatter(7)
         round_into_words(7, 2)
+        nc.scalar.activation(woven1[2][:, :SHARED_CUT, 3], planes[7][:, 2 * BANK : 2 * BANK + SHARED_CUT], ACT.Copy)
 
         page1_codes, page1_sc = {}, {}
 
@@ -219,7 +226,7 @@ def tile_list_mine_loop_closure_kernel(
         nc.vector.tensor_copy(woven1[3][:, :, 3], planes[7][:, 3 * BANK : 4 * BANK])
         quantise_pass1(0)
         quantise_pass0(0, BANK, 2 * BANK)
-        nc.vector.tensor_copy(woven1[2][:, :, 3], planes[7][:, 2 * BANK : 3 * BANK])
+        nc.vector.tensor_copy(woven1[2][:, SHARED_CUT:, 3], planes[7][:, 2 * BANK + SHARED_CUT : 3 * BANK])
         quantise_pass1(1)
         quantise_pass0(1, 0, 2 * BANK)
         quantise_pass1(3)

@@ -55,7 +55,10 @@ def tile_list_mine_loop_closure_kernel(
         slot_list = lists.tile([P, LIST_COLS], U16, name="slot_list")
         pair_list = lists.tile([P, LIST_COLS], U16, name="pair_list")
         tab_sc = sbuf([P, T], U8, "tab_sc")
-        nc.vector.memset(tab_sc[:].bitcast(I32), 0)
+        nc.vector.memset(tab_sc[32:64, :].bitcast(I32), 0)
+        nc.vector.memset(tab_sc[64:, :].bitcast(I32), 0)
+        v_sc = sbuf([P, S], U8, "v_sc")
+        nc.gpsimd.memset(v_sc[:].bitcast(I32), 0)
         w4_sc = sbuf([P, N], U8, "w4_sc")
         nc.gpsimd.memset(w4_sc[:].bitcast(I32), 0)
         nc.sync.dma_start(tab_list[:], offs)
@@ -66,13 +69,9 @@ def tile_list_mine_loop_closure_kernel(
             xs_rows = xs[g * K_PASS : (g + 1) * K_PASS, :].rearrange("(p i) m -> p i m", i=PACK)[:, i, :]
             nc.sync.dma_start(news[n][:, first:last], xs_rows[:, first:last])
 
-        for q in range(QUADRANTS):
-            nc.sync.dma_start(
-                tab_sc[32 * q : 32 * q + 4 * PASSES, :].bitcast(I32), tab_scales[:, 4 * q : 4 * q + 4, :].bitcast(I32)
-            )
-        nc.sync.dma_start(slot_list[:], offs2)
-        v_sc = sbuf([P, S], U8, "v_sc")
-        nc.vector.tensor_copy(v_sc[:], tab_sc[:].indirect(tab_list[:]))
+        nc.sync.dma_start(tab_sc[:32, :].bitcast(I32), tab_scales.rearrange("g q t -> (g q) t").bitcast(I32))
+        picked_sc = sbuf([P, S], U8, "picked_sc")
+        nc.vector.tensor_copy(picked_sc[:], tab_sc[:].indirect(tab_list[:]))
 
         planes = []
 
@@ -82,6 +81,7 @@ def tile_list_mine_loop_closure_kernel(
             nc.sync.dma_start(plane[:], base[g * K_PASS : (g + 1) * K_PASS, :].rearrange("(p i) t -> p i t", i=PACK)[:, i, :])
             if first_new:
                 load_new(n, 0, first_new)
+                nc.sync.dma_start(slot_list[:], offs2)
             load_new(n, first_new, S)
             planes.append(plane)
 
@@ -103,6 +103,10 @@ def tile_list_mine_loop_closure_kernel(
         load_plane(6, 0)
         load_plane(7, 0)
         nc.sync.dma_start(pair_list[:], offs3)
+        for g in range(PASSES):
+            for q in range(QUADRANTS):
+                src, dst = 16 * g + 4 * q, 32 * q + 4 * g
+                nc.sync.dma_start(v_sc[dst : dst + 4, :].bitcast(I32), picked_sc[src : src + 4, :].bitcast(I32))
         decay_sb = sbuf([P, PACK], F32, "decay_sb")
         gain_sb = sbuf([P, PACK], F32, "gain_sb")
         bias_sb = sbuf([P, N // P], F32, "bias_sb")

@@ -100,13 +100,18 @@ def tile_list_mine_loop_closure_kernel(
             words = sbuf([P, T], I32, "tab%d" % g)
             nc.sync.dma_start(words[:], tab_hbm[g])
             tab.append(words)
+
+
+        def move_scale_rows(g, q):
+            src, dst = 16 * g + 4 * q, 32 * q + 4 * g
+            nc.sync.dma_start(v_sc[dst : dst + 4, :].bitcast(I32), picked_sc[src : src + 4, :].bitcast(I32))
+
         load_plane(6, 0)
+        for n in range(PASSES * QUADRANTS - 1):
+            move_scale_rows(*divmod(n, QUADRANTS))
         load_plane(7, 0)
+        move_scale_rows(PASSES - 1, QUADRANTS - 1)
         nc.sync.dma_start(pair_list[:], offs3)
-        for g in range(PASSES):
-            for q in range(QUADRANTS):
-                src, dst = 16 * g + 4 * q, 32 * q + 4 * g
-                nc.sync.dma_start(v_sc[dst : dst + 4, :].bitcast(I32), picked_sc[src : src + 4, :].bitcast(I32))
         decay_sb = sbuf([P, PACK], F32, "decay_sb")
         gain_sb = sbuf([P, PACK], F32, "gain_sb")
         bias_sb = sbuf([P, N // P], F32, "bias_sb")
@@ -191,7 +196,7 @@ def tile_list_mine_loop_closure_kernel(
 
         page1_codes, page1_sc = {}, {}
 
-        held_sc = sbuf([P, 3, PAGE_HALF], U8, "held_sc", "new7")
+        held_sc = sbuf([P, 2, PAGE_HALF], U8, "held_sc", "new7")
 
         page0_codes = [sbuf([P, PAGE_HALF], U32, "page0_codes%d" % h) for h in range(2)]
         page0_sc = [held_sc[:, h, :] for h in range(2)]
@@ -218,7 +223,7 @@ def tile_list_mine_loop_closure_kernel(
             return words
 
         w1_codes = sbuf([P, PASSES * H], U32, "w1_codes", "new6")
-        w1_sc = held_sc[:, 2, :]
+        w1_sc = sbuf([P, PASSES * H], U8, "w1_sc", "picked_sc")
 
         def quantise_w1(g):
             cols = slice(g * H, (g + 1) * H)
@@ -310,7 +315,7 @@ def tile_list_mine_loop_closure_kernel(
         def product_with_w4(n, z, width, codes_tag):
             codes = sbuf([P, width], U32, "z_codes%d" % n, codes_tag)
             scales = sbuf([P, width], U8, "z_sc%d" % n)
-            nc.vector.quantize_mx(out=codes[:].bitcast(FP8X4), scales=scales[:], in_=z[:].rearrange("p c t -> p (c t)"))
+            nc.vector.quantize_mx(out=codes[:].bitcast(FP8X4), scales=scales[:], in_=z.rearrange("p c t -> p (c t)"))
 
             def rows(u, acc=None):
                 if acc is None:
@@ -360,19 +365,22 @@ def tile_list_mine_loop_closure_kernel(
         z0 = sbuf([P, BANK, PACK], BF16, "z0", "plane2")
         for q in range(2):
             weigh(z0[:, q * quarter : (q + 1) * quarter, :], sim0[q])
-        votes0 = product_with_w4(0, z0, BANK, "z_codes0")
+        votes0 = [product_with_w4(0, z0[:, :quarter, :], quarter, "z_codes0")]
         z1 = sbuf([P, quarter, PACK], BF16, "z1", "b0")
         weigh(z1[:], sim1)
+        votes0.append(product_with_w4(4, z0[:, quarter:, :], quarter, "z_codes4"))
         z2 = sbuf([P, P, PACK], BF16, "z2", "new1")
         weigh(z2[:], sim2)
-        votes1 = product_with_w4(1, z1, quarter, rate_parts[2][2])
+        votes1 = product_with_w4(1, z1[:], quarter, rate_parts[2][2])
         z3 = sbuf([P, P, PACK], BF16, "z3")
         weigh(z3[:], sim3)
-        votes2 = product_with_w4(2, z2, P, rate_parts[3][2])
-        votes3 = product_with_w4(3, z3, P, "z_codes3")
+        votes2 = product_with_w4(2, z2[:], P, rate_parts[3][2])
+        votes3 = product_with_w4(3, z3[:], P, "z_codes3")
         for u in range(N // P):
-            acc = votes0(u)
-            store_by_scalar(acc, sbuf([P, BANK], F32, "res0_%d" % u, ("woven0_0", "new0")[u]), u, 0, nc.sync)
+            acc = next_bank()
+            for q in range(2):
+                votes0[q](u, acc[:, q * quarter : (q + 1) * quarter])
+            store_by_scalar(acc[:], sbuf([P, BANK], F32, "res0_%d" % u, ("woven0_0", "new0")[u]), u, 0, nc.sync)
         for u in range(N // P):
             acc = votes1(u)
             store_by_scalar(acc, sbuf([P, quarter], F32, "res1_%d" % u), u, BANK, nc.sync)

@@ -92,7 +92,8 @@ def tile_list_mine_loop_closure_kernel(
             raw = sbuf([P, PACK, H], F32, "w1_raw%d" % g)
             nc.sync.dma_start(raw[:], w1[g * K_PASS : (g + 1) * K_PASS, :].rearrange("(p i) r -> p i r", i=PACK))
             w1_raw.append(raw)
-        for n in range(2, 6):
+            load_plane(2 + g, 0)
+        for n in range(4, 6):
             load_plane(n, 0)
         tab_hbm = [tab_words[g].rearrange("p t i -> p (t i)").bitcast(I32) for g in range(PASSES)]
         tab = []

@@ -135,13 +135,13 @@ def tile_list_mine_loop_closure_kernel(
         def round_into_pairs(n):
             u, e = divmod(n % PACK, 2)
             for h in range(2):
-                nc.scalar.activation(pairs[h][:, u, :, e], planes[n][:, h * PAGE_HALF : (h + 1) * PAGE_HALF], ACT.Copy)
+                nc.scalar.copy(pairs[h][:, u, :, e], planes[n][:, h * PAGE_HALF : (h + 1) * PAGE_HALF])
 
         woven1 = [sbuf([P, BANK, PACK], BF16, "woven1_%d" % c) for c in range(CHUNKS)]
 
         def round_into_words(n, chunks):
             for c in range(chunks):
-                nc.scalar.activation(woven1[c][:, :, n - PACK], planes[n][:, c * BANK : (c + 1) * BANK], ACT.Copy)
+                nc.scalar.copy(woven1[c][:, :, n - PACK], planes[n][:, c * BANK : (c + 1) * BANK])
 
         for first, last in ((0, FIRST_CUT), (FIRST_CUT, S)):
             nc.vector.tensor_copy(planes[0][:].indirect(slot_list[:, first // 16 : last // 16]), news[0][:, first:last])
@@ -186,14 +186,14 @@ def tile_list_mine_loop_closure_kernel(
             ALU.mult,
             ALU.add,
         )
-        nc.scalar.activation(pairs[1][:, 1, BANK:, 0], planes[6][:, T - BANK :], ACT.Copy)
+        nc.scalar.copy(pairs[1][:, 1, BANK:, 0], planes[6][:, T - BANK :])
         nc.scalar.copy(
             words_of(CHUNKS - 1),
             pairs[1][:, :, BANK:, :].rearrange("p u c e -> p u (c e)").bitcast(F32).rearrange("p u c -> p c u"),
         )
         scatter(7)
         round_into_words(7, 2)
-        nc.scalar.activation(woven1[2][:, :SHARED_CUT, 3], planes[7][:, 2 * BANK : 2 * BANK + SHARED_CUT], ACT.Copy)
+        nc.scalar.copy(woven1[2][:, :SHARED_CUT, 3], planes[7][:, 2 * BANK : 2 * BANK + SHARED_CUT])
 
         page1_codes, page1_sc = {}, {}
 
@@ -269,7 +269,7 @@ def tile_list_mine_loop_closure_kernel(
             h, part = divmod(c, 2)
             cols = slice(part * BANK, (part + 1) * BANK)
             project(acc, t, [(page0_codes[h][:, cols], page0_sc[h][:, cols]), (page1_codes[c][:], page1_sc[c][:])])
-            nc.scalar.activation(a_sb[t][:, c * BANK : (c + 1) * BANK], acc[:], ACT.Copy)
+            nc.scalar.copy(a_sb[t][:, c * BANK : (c + 1) * BANK], acc[:])
 
         diff = [sbuf([P, PACK, BANK], F32, "dist%d" % h, "pairs%d" % h) for h in range(2)]
         rate_parts = (
@@ -285,7 +285,7 @@ def tile_list_mine_loop_closure_kernel(
             cols = slice(h * BANK, (h + 1) * BANK)
             project(acc, t, [(v_words[g, h][:], v_sc[4 * g :, cols]) for g in range(PASSES)])
             b_sb = sbuf([P, BANK], F32, "b%d_%d" % (t, h), tag)
-            nc.scalar.activation(b_sb[:], acc[:], ACT.Copy)
+            nc.scalar.copy(b_sb[:], acc[:])
             return b_sb
 
         def gather_minus_b(t, h, b_sb):
@@ -382,9 +382,10 @@ def tile_list_mine_loop_closure_kernel(
             for q in range(2):
                 votes0[q](u, acc[:, q * quarter : (q + 1) * quarter])
             store_by_scalar(acc[:], sbuf([P, BANK], F32, "res0_%d" % u, ("woven0_0", "new0")[u]), u, 0, nc.sync)
-        for u in range(N // P):
-            acc = votes1(u)
-            store_by_scalar(acc, sbuf([P, quarter], F32, "res1_%d" % u), u, BANK, nc.sync)
+        store_by_scalar(votes1(0), sbuf([P, quarter], F32, "res1_0"), 0, BANK, nc.sync)
+        res = sbuf([P, quarter], F32, "res1_1", "z3")
+        nc.vector.tensor_scalar(res[:], votes1(1), bias_sb[:, 1:2], None, ALU.add)
+        nc.sync.dma_start(out[P : 2 * P, BANK : BANK + quarter], res[:])
         j_last = BANK + quarter
         last = [next_bank(), next_bank()]
         for votes, c0 in ((votes2, 0), (votes3, P)):

@@ -69,7 +69,7 @@ def tile_list_mine_loop_closure_kernel(
             xs_rows = xs[g * K_PASS : (g + 1) * K_PASS, :].rearrange("(p i) m -> p i m", i=PACK)[:, i, :]
             nc.sync.dma_start(news[n][:, first:last], xs_rows[:, first:last])
 
-        nc.sync.dma_start(tab_sc[:32, :].bitcast(I32), tab_scales.rearrange("g q t -> (g q) t").bitcast(I32))
+        nc.scalar.dma_start(tab_sc[:32, :].bitcast(I32), tab_scales.rearrange("g q t -> (g q) t").bitcast(I32))
         picked_sc = sbuf([P, S], U8, "picked_sc")
         nc.vector.tensor_copy(picked_sc[:], tab_sc[:].indirect(tab_list[:]))
 

@@ -64,10 +64,10 @@ def tile_list_mine_loop_closure_kernel(
         nc.sync.dma_start(tab_list[:], offs)
         news = [sbuf([P, S], F32, "new%d" % n) for n in range(PASSES * PACK)]
 
-        def load_new(n, first, last):
+        def load_new(n, first, last, queue=nc.sync):
             g, i = divmod(n, PACK)
             xs_rows = xs[g * K_PASS : (g + 1) * K_PASS, :].rearrange("(p i) m -> p i m", i=PACK)[:, i, :]
-            nc.sync.dma_start(news[n][:, first:last], xs_rows[:, first:last])
+            queue.dma_start(news[n][:, first:last], xs_rows[:, first:last])
 
         nc.scalar.dma_start(tab_sc[:32, :].bitcast(I32), tab_scales.rearrange("g q t -> (g q) t").bitcast(I32))
         picked_sc = sbuf([P, S], U8, "picked_sc")
@@ -78,10 +78,10 @@ def tile_list_mine_loop_closure_kernel(
         def load_plane(n, first_new):
             g, i = divmod(n, PACK)
             plane = sbuf([P, T], F32, "plane%d" % n)
-            nc.sync.dma_start(plane[:], base[g * K_PASS : (g + 1) * K_PASS, :].rearrange("(p i) t -> p i t", i=PACK)[:, i, :])
             if first_new:
-                load_new(n, 0, first_new)
+                load_new(n, 0, first_new, nc.scalar)
                 nc.sync.dma_start(slot_list[:], offs2)
+            nc.sync.dma_start(plane[:], base[g * K_PASS : (g + 1) * K_PASS, :].rearrange("(p i) t -> p i t", i=PACK)[:, i, :])
             load_new(n, first_new, S)
             planes.append(plane)
 

@@ -44,9 +44,11 @@ def tile_list_mine_loop_closure_kernel(
 
         banks = []
 
-        def next_bank():
-            banks.append(psum.tile([P, BANK], F32, name="bank%d" % (len(banks) % PSUM_BANKS)))
-            return banks[-1]
+        def next_bank(number=None):
+            if number is None:
+                number = (banks[-1] + 1) % PSUM_BANKS if banks else 0
+            banks.append(number)
+            return psum.tile([P, BANK], F32, name="bank%d" % number)
 
         def list_half(tile, h):
             return tile[:, h * LIST_COLS // 2 : (h + 1) * LIST_COLS // 2]
@@ -130,6 +132,9 @@ def tile_list_mine_loop_closure_kernel(
         def scatter(n):
             nc.vector.tensor_copy(planes[n][:].indirect(slot_list[:]), news[n][:])
 
+        def chunk(c):
+            return slice(c * BANK, (c + 1) * BANK)
+
         pairs = [sbuf([P, 2, PAGE_HALF, 2], BF16, "pairs%d" % h) for h in range(2)]
 
         def round_into_pairs(n):
@@ -137,76 +142,72 @@ def tile_list_mine_loop_closure_kernel(
             for h in range(2):
                 nc.scalar.copy(pairs[h][:, u, :, e], planes[n][:, h * PAGE_HALF : (h + 1) * PAGE_HALF])
 
-        woven1 = [sbuf([P, BANK, PACK], BF16, "woven1_%d" % c) for c in range(CHUNKS)]
-
-        def round_into_words(n, chunks):
-            for c in range(chunks):
-                nc.scalar.copy(woven1[c][:, :, n - PACK], planes[n][:, c * BANK : (c + 1) * BANK])
-
         for first, last in ((0, FIRST_CUT), (FIRST_CUT, S)):
             nc.vector.tensor_copy(planes[0][:].indirect(slot_list[:, first // 16 : last // 16]), news[0][:, first:last])
         round_into_pairs(0)
-        w1_woven = sbuf([P, PASSES, PACK * H], BF16, "w1_bf")
+        w1_woven = []
         for g in range(PASSES):
+            woven = sbuf([P, PACK * H], BF16, "w1_bf%d" % g)
             nc.scalar.activation(
-                w1_woven[:, g, :].rearrange("p (t m i) -> p m i t", t=PACK, i=PACK),
+                woven[:].rearrange("p (t m i) -> p m i t", t=PACK, i=PACK),
                 w1_raw[g][:].rearrange("p i (m t) -> p m i t", t=PACK),
                 ACT.Copy,
             )
+            w1_woven.append(woven)
         for n in range(1, PACK):
             scatter(n)
             round_into_pairs(n)
         woven0 = []
-        for h in range(2):
-            woven = sbuf([P, PAGE_HALF * PACK], BF16, "woven0_%d" % h)
+        for c in range(CHUNKS):
+            h, part = divmod(c, 2)
+            woven = sbuf([P, BANK * PACK], BF16, "woven0_%d" % c)
             nc.scalar.copy(
                 woven[:].bitcast(F32).rearrange("p (c u) -> p c u", u=2),
-                pairs[h][:].rearrange("p u c e -> p u (c e)").bitcast(F32).rearrange("p u c -> p c u"),
+                pairs[h][:, :, chunk(part), :].rearrange("p u c e -> p u (c e)").bitcast(F32).rearrange("p u c -> p c u"),
             )
             woven0.append(woven)
 
+        woven1 = [sbuf([P, BANK, PACK], BF16, "woven1_%d" % c) for c in range(CHUNKS)]
         for n in (4, 5):
             scatter(n)
             round_into_pairs(n)
+
         def words_of(c):
             return woven1[c][:].rearrange("p c i -> p (c i)").bitcast(F32).rearrange("p (c u) -> p c u", u=2)
 
-        for c in range(CHUNKS - 1):
+        for c in (3, 0, 1):
             h, part = divmod(c, 2)
-            nc.scalar.copy(
-                words_of(c), pairs[h][:, 0, part * BANK : (part + 1) * BANK, :].bitcast(F32).to_broadcast([P, BANK, 2])
-            )
+            nc.scalar.copy(words_of(c), pairs[h][:, 0, chunk(part), :].bitcast(F32).to_broadcast([P, BANK, 2]))
+
+        def weave_on_scalar(n, c):
+            nc.scalar.copy(woven1[c][:, :, n - PACK], planes[n][:, chunk(c)])
+
+        def weave_on_gpsimd(n, c, one):
+            nc.gpsimd.tensor_scalar(woven1[c][:, :, n - PACK], planes[n][:, chunk(c)], one, 0.0, ALU.mult, ALU.add)
+
         scatter(6)
-        round_into_words(6, 2)
-        nc.gpsimd.tensor_scalar(
-            woven1[2][:, :, 2:4],
-            planes[6][:, 2 * BANK : 3 * BANK].unsqueeze(2).to_broadcast([P, BANK, 2]),
-            1.0,
-            0.0,
-            ALU.mult,
-            ALU.add,
-        )
-        nc.scalar.copy(pairs[1][:, 1, BANK:, 0], planes[6][:, T - BANK :])
+        weave_on_gpsimd(6, 3, 1.0)
+        for c in (0, 1):
+            weave_on_scalar(6, c)
+        nc.scalar.copy(pairs[1][:, 1, :BANK, 0], planes[6][:, chunk(2)])
         nc.scalar.copy(
-            words_of(CHUNKS - 1),
-            pairs[1][:, :, BANK:, :].rearrange("p u c e -> p u (c e)").bitcast(F32).rearrange("p u c -> p c u"),
+            words_of(2),
+            pairs[1][:, :, :BANK, :].rearrange("p u c e -> p u (c e)").bitcast(F32).rearrange("p u c -> p c u"),
         )
         scatter(7)
-        round_into_words(7, 2)
+        for c in (0, 1):
+            weave_on_scalar(7, c)
         nc.scalar.copy(woven1[2][:, :SHARED_CUT, 3], planes[7][:, 2 * BANK : 2 * BANK + SHARED_CUT])
 
         page1_codes, page1_sc = {}, {}
-
         held_sc = sbuf([P, 2, PAGE_HALF], U8, "held_sc", "new7")
-
-        page0_codes = [sbuf([P, PAGE_HALF], U32, "page0_codes%d" % h) for h in range(2)]
+        page0_codes = [sbuf([P, PAGE_HALF], U32, "page0_codes0")]
         page0_sc = [held_sc[:, h, :] for h in range(2)]
 
-        def quantise_pass0(h, first, last):
+        def quantise_pass0(c):
+            h, part = divmod(c, 2)
             nc.vector.quantize_mx(
-                out=page0_codes[h][:, first:last].bitcast(FP8X4),
-                scales=page0_sc[h][:, first:last],
-                in_=woven0[h][:, PACK * first : PACK * last],
+                out=page0_codes[h][:, chunk(part)].bitcast(FP8X4), scales=page0_sc[h][:, chunk(part)], in_=woven0[c][:]
             )
 
         def quantise_pass1(c):
@@ -217,35 +218,39 @@ def tile_list_mine_loop_closure_kernel(
             )
             page1_codes[c], page1_sc[c] = codes, scales
 
-        def gather_words(g, entries, name, tag):
-            words = sbuf([P, len(entries)], U32, name, tag)
-            offsets = tab_list[:, entries.start // 16 : entries.stop // 16]
-            nc.vector.tensor_copy(words[:], tab[g][:].bitcast(U32).indirect(offsets))
-            return words
+        v_words = {}
+
+        def gather_words(g, h, tag):
+            words = sbuf([P, BANK], U32, "v%d_%d" % (g, h), tag)
+            nc.vector.tensor_copy(words[:], tab[g][:].bitcast(U32).indirect(list_half(tab_list, h)))
+            v_words[g, h] = words
 
         w1_codes = sbuf([P, PASSES * H], U32, "w1_codes", "new6")
         w1_sc = sbuf([P, PASSES * H], U8, "w1_sc", "picked_sc")
 
         def quantise_w1(g):
             cols = slice(g * H, (g + 1) * H)
-            nc.vector.quantize_mx(out=w1_codes[:, cols].bitcast(FP8X4), scales=w1_sc[:, cols], in_=w1_woven[:, g, :])
+            nc.vector.quantize_mx(out=w1_codes[:, cols].bitcast(FP8X4), scales=w1_sc[:, cols], in_=w1_woven[g][:])
 
         quantise_w1(0)
-        quantise_pass0(0, 0, BANK)
+        quantise_pass0(0)
         quantise_w1(1)
-        nc.vector.tensor_copy(woven1[3][:, :, 3], planes[7][:, 3 * BANK : 4 * BANK])
+        quantise_pass0(1)
         quantise_pass1(0)
-        quantise_pass0(0, BANK, 2 * BANK)
-        nc.vector.tensor_copy(woven1[2][:, SHARED_CUT:, 3], planes[7][:, 2 * BANK + SHARED_CUT : 3 * BANK])
+        one = sbuf([P, 1], F32, "one", "woven1_0")
+        nc.gpsimd.memset(one[:], 1.0)
+        weave_on_gpsimd(7, 3, one[:, 0:1])
+        gather_words(0, 0, "w1_bf1")
+        gather_words(1, 0, "w1_bf0")
+        gather_words(0, 1, "woven0_0")
         quantise_pass1(1)
-        quantise_pass0(1, 0, 2 * BANK)
-        quantise_pass1(3)
+        nc.vector.tensor_copy(woven1[2][:, SHARED_CUT:, 3], planes[7][:, 2 * BANK + SHARED_CUT : 3 * BANK])
+        page0_codes.append(sbuf([P, PAGE_HALF], U32, "page0_codes1", "woven1_0"))
+        quantise_pass0(2)
         quantise_pass1(2)
-        word_tags = {(0, 0): "woven1_1", (1, 0): "woven1_3", (0, 1): "woven1_2", (1, 1): "woven0_1"}
-        v_words = {}
-        for h in range(2):
-            for g in range(PASSES):
-                v_words[g, h] = gather_words(g, range(h * BANK, (h + 1) * BANK), "v%d_%d" % (g, h), word_tags[g, h])
+        quantise_pass0(3)
+        quantise_pass1(3)
+        gather_words(1, 1, "woven0_3")
 
         def project(acc, t, moving):
             for g in range(PASSES):
@@ -261,27 +266,26 @@ def tile_list_mine_loop_closure_kernel(
                     stop=(g == PASSES - 1),
                 )
 
-        a_tags = ("plane0", "plane1", "plane2", "plane3")
-        a_sb = [sbuf([P, T], F32, "a%d" % t, a_tags[t]) for t in range(PACK)]
+        a_sb = [sbuf([P, T], F32, "a%d" % t, "plane%d" % t) for t in range(PACK)]
 
-        def project_page(t, c):
-            acc = next_bank()
+        def project_page(t, c, copy=nc.scalar.copy, bank=None):
+            acc = next_bank(bank)
             h, part = divmod(c, 2)
             cols = slice(part * BANK, (part + 1) * BANK)
             project(acc, t, [(page0_codes[h][:, cols], page0_sc[h][:, cols]), (page1_codes[c][:], page1_sc[c][:])])
-            nc.scalar.copy(a_sb[t][:, c * BANK : (c + 1) * BANK], acc[:])
+            copy(a_sb[t][:, chunk(c)], acc[:])
 
         diff = [sbuf([P, PACK, BANK], F32, "dist%d" % h, "pairs%d" % h) for h in range(2)]
         rate_parts = (
-            (0, BANK, "page1_codes2"),
-            (BANK, 2 * P, "page0_codes1"),
+            (0, BANK, "page1_codes3"),
+            (BANK, 2 * P, "woven1_0"),
             (S - 2 * P, P, "rate2"),
             (S - P, P, "rate3"),
         )
         rate = [sbuf([P, PACK, width], F32, "rate%d" % n, tag) for n, (j0, width, tag) in enumerate(rate_parts)]
 
-        def fetch_b(t, h, tag):
-            acc = next_bank()
+        def fetch_b(t, h, tag, bank=None):
+            acc = next_bank(bank)
             cols = slice(h * BANK, (h + 1) * BANK)
             project(acc, t, [(v_words[g, h][:], v_sc[4 * g :, cols]) for g in range(PASSES)])
             b_sb = sbuf([P, BANK], F32, "b%d_%d" % (t, h), tag)
@@ -338,18 +342,24 @@ def tile_list_mine_loop_closure_kernel(
             nc.scalar.activation(res[:], acc, ACT.Identity, bias=bias_sb[:, u : u + 1])
             queue.dma_start(out[u * P : (u + 1) * P, j0 : j0 + res.shape[1]], res[:])
 
-        for c in (0, 1):
-            for t in range(PACK):
-                project_page(t, c)
         b_sb = {}
-        for tiles in ((0, 1), (2,), (3,)):
-            for t in tiles:
-                for c in (3, 2):
-                    project_page(t, c)
-            for t in tiles:
-                b_sb[t, 0] = fetch_b(t, 0, "b%d" % t)
         for t in range(PACK):
-            b_sb[t, 1] = fetch_b(t, 1, "new%d" % (2 + t))
+            project_page(t, 0)
+        for t in range(PACK):
+            b_sb[t, 0] = fetch_b(t, 0, "new%d" % (2 + t))
+        for t in range(PACK - 1):
+            project_page(t, 1)
+        project_page(0, 2, bank=3)
+        project_page(2, 2)
+        project_page(0, 3)
+        project_page(1, 2, copy=nc.vector.tensor_copy)
+        project_page(1, 3)
+        project_page(2, 3)
+        project_page(3, 1, bank=3)
+        project_page(3, 2, bank=1)
+        project_page(3, 3)
+        for t in range(PACK):
+            b_sb[t, 1] = fetch_b(t, 1, "b%d" % t, 4 + t)
         for h in range(2):
             for t in range(PACK):
                 gather_minus_b(t, h, b_sb[t, h])

@@ -26,7 +26,7 @@ PSUM_BANKS = 8
 CHUNKS = T // BANK
 PAGE_HALF = T // 2
 LIST_COLS = S // 16
-SHARED_CUT = BANK // 2
+SHARED_CUT = P
 FIRST_CUT = S // 4
 
 
@@ -252,8 +252,8 @@ def tile_list_mine_loop_closure_kernel(
         quantise_pass1(3)
         gather_words(1, 1, "woven0_3")
 
-        def project(acc, t, moving):
-            for g in range(PASSES):
+        def project(acc, t, moving, passes=range(PASSES)):
+            for g in passes:
                 cols = slice(g * H + t * P, g * H + (t + 1) * P)
                 codes, scales = moving[g]
                 nc.tensor.matmul_mx(
@@ -284,10 +284,12 @@ def tile_list_mine_loop_closure_kernel(
         )
         rate = [sbuf([P, PACK, width], F32, "rate%d" % n, tag) for n, (j0, width, tag) in enumerate(rate_parts)]
 
+        def table_operands(h):
+            return [(v_words[g, h][:], v_sc[4 * g :, chunk(h)]) for g in range(PASSES)]
+
         def fetch_b(t, h, tag, bank=None):
             acc = next_bank(bank)
-            cols = slice(h * BANK, (h + 1) * BANK)
-            project(acc, t, [(v_words[g, h][:], v_sc[4 * g :, cols]) for g in range(PASSES)])
+            project(acc, t, table_operands(h))
             b_sb = sbuf([P, BANK], F32, "b%d_%d" % (t, h), tag)
             nc.scalar.copy(b_sb[:], acc[:])
             return b_sb
@@ -345,8 +347,14 @@ def tile_list_mine_loop_closure_kernel(
         b_sb = {}
         for t in range(PACK):
             project_page(t, 0)
+        first_b = [next_bank() for t in range(PACK)]
+        for step in range(PACK + 1):
+            for g in range(PASSES):
+                if 0 <= step - g < PACK:
+                    project(first_b[step - g], step - g, table_operands(0), (g,))
         for t in range(PACK):
-            b_sb[t, 0] = fetch_b(t, 0, "new%d" % (2 + t))
+            b_sb[t, 0] = sbuf([P, BANK], F32, "b%d_0" % t, "new%d" % (2 + t))
+            nc.scalar.copy(b_sb[t, 0][:], first_b[t][:])
         for t in range(PACK - 1):
             project_page(t, 1)
         project_page(0, 2, bank=3)

@@ -167,13 +167,15 @@ def tile_list_mine_loop_closure_kernel(
             )
             woven0.append(woven)
 
-        woven1 = [sbuf([P, BANK, PACK], BF16, "woven1_%d" % c) for c in range(CHUNKS)]
+        woven1 = [sbuf([P, BANK, PACK], BF16, "woven1_%d" % c)[:] for c in range(2)]
+        second_half = sbuf([P, PAGE_HALF, PACK], BF16, "woven1_half")
+        woven1.extend(second_half[:, chunk(part), :] for part in range(2))
         for n in (4, 5):
             scatter(n)
             round_into_pairs(n)
 
         def words_of(c):
-            return woven1[c][:].rearrange("p c i -> p (c i)").bitcast(F32).rearrange("p (c u) -> p c u", u=2)
+            return woven1[c].rearrange("p c i -> p (c i)").bitcast(F32).rearrange("p (c u) -> p c u", u=2)
 
         for c in (3, 0, 1):
             h, part = divmod(c, 2)
@@ -214,7 +216,7 @@ def tile_list_mine_loop_closure_kernel(
             codes = sbuf([P, BANK], U32, "page1_codes%d" % c)
             scales = sbuf([P, BANK], U8, "page1_sc%d" % c)
             nc.vector.quantize_mx(
-                out=codes[:].bitcast(FP8X4), scales=scales[:], in_=woven1[c][:].rearrange("p c i -> p (c i)")
+                out=codes[:].bitcast(FP8X4), scales=scales[:], in_=woven1[c].rearrange("p c i -> p (c i)")
             )
             page1_codes[c], page1_sc[c] = codes, scales
 
@@ -239,12 +241,17 @@ def tile_list_mine_loop_closure_kernel(
         quantise_pass1(0)
         one = sbuf([P, 1], F32, "one", "woven1_0")
         nc.gpsimd.memset(one[:], 1.0)
-        weave_on_gpsimd(7, 3, one[:, 0:1])
+        nc.gpsimd.tensor_tensor(
+            second_half[:, 2 * P :, 3],
+            planes[7][:, PAGE_HALF + 2 * P :],
+            one[:].to_broadcast([P, PAGE_HALF - 2 * P]),
+            ALU.mult,
+        )
         gather_words(0, 0, "w1_bf1")
         gather_words(1, 0, "w1_bf0")
         gather_words(0, 1, "woven0_0")
         quantise_pass1(1)
-        nc.vector.tensor_copy(woven1[2][:, SHARED_CUT:, 3], planes[7][:, 2 * BANK + SHARED_CUT : 3 * BANK])
+        nc.vector.tensor_copy(woven1[2][:, P : 2 * P, 3], planes[7][:, 2 * BANK + P : 2 * BANK + 2 * P])
         page0_codes.append(sbuf([P, PAGE_HALF], U32, "page0_codes1", "woven1_0"))
         quantise_pass0(2)
         quantise_pass1(2)

@@ -40,7 +40,7 @@ def tile_list_mine_loop_closure_kernel(
         psum = ctx.enter_context(tc.psum_pool(name="psum", bufs=1))
 
         def sbuf(shape, dtype, name, tag=None):
-            return sb.tile(shape, dtype, name=name, tag=tag or name, align_bytes=64)
+            return sb.tile(shape, dtype, name=name, tag=tag or name, align_bytes=256)
 
         banks = []
 
@@ -374,7 +374,7 @@ def tile_list_mine_loop_closure_kernel(
         project_page(3, 2, bank=1)
         project_page(3, 3)
         for t in range(PACK):
-            b_sb[t, 1] = fetch_b(t, 1, "b%d" % t, 4 + t)
+            b_sb[t, 1] = fetch_b(t, 1, ("b0", "plane4", "plane5", "plane6")[t], 4 + t)
         for h in range(2):
             for t in range(PACK):
                 gather_minus_b(t, h, b_sb[t, h])
@@ -387,7 +387,7 @@ def tile_list_mine_loop_closure_kernel(
         scale_distances(2)
         scale_distances(3)
         sim2 = similarity(3, 2, 0, P, "new0")
-        sim3 = similarity(4, 3, 0, P, "sim4")
+        sim3 = similarity(4, 3, 0, P, "plane7")
         z0 = sbuf([P, BANK, PACK], BF16, "z0", "plane2")
         for q in range(2):
             weigh(z0[:, q * quarter : (q + 1) * quarter, :], sim0[q])
@@ -416,7 +416,7 @@ def tile_list_mine_loop_closure_kernel(
         for votes, c0 in ((votes2, 0), (votes3, P)):
             for u in range(N // P):
                 votes(u, last[u][:, c0 : c0 + P])
-        store_by_scalar(last[0][:, :quarter], sbuf([P, quarter], F32, "res2_0"), 0, j_last, nc.scalar)
-        res = sbuf([P, quarter], F32, "res2_1")
+        store_by_scalar(last[0][:, :quarter], sbuf([P, quarter], F32, "res2_0", "tab0"), 0, j_last, nc.scalar)
+        res = sbuf([P, quarter], F32, "res2_1", "tab1")
         nc.vector.tensor_scalar(res[:], last[1][:, :quarter], bias_sb[:, 1:2], None, ALU.add)
         nc.sync.dma_start(out[P : 2 * P, j_last : j_last + quarter], res[:])

from contextlib import ExitStack

import concourse.mybir as mybir

K, T, S, H, N = 1024, 2048, 1024, 512, 256
FLOPS = 2 * K * H * T + 2 * K * H * S + 2 * H * N * S

F32 = mybir.dt.float32
BF16 = mybir.dt.bfloat16
I32 = mybir.dt.int32
U32 = mybir.dt.uint32
U16 = mybir.dt.uint16
U8 = mybir.dt.uint8
FP8X4 = mybir.dt.float8_e4m3fn_x4
FP4X4 = mybir.dt.float4_e2m1fn_x4
ACT = mybir.ActivationFunctionType
ALU = mybir.AluOpType

P = 128
PACK = 4
K_PASS = P * PACK
PASSES = K // K_PASS
QUADRANTS = 4
BANK = 512
PSUM_BANKS = 8
CHUNKS = T // BANK
PAGE_HALF = T // 2
LIST_COLS = S // 16
SHARED_CUT = P
FIRST_CUT = S // 4


def tile_list_mine_loop_closure_kernel(
    tc, tab_words, tab_scales, offs, offs2, offs3, xs, base, w1, decay, gain, w4_words, w4_scales, bias, out
):
    nc = tc.nc
    with ExitStack() as ctx:
        lists = ctx.enter_context(tc.tile_pool(name="lists", bufs=1))
        sb = ctx.enter_context(tc.tile_pool(name="sb", bufs=1))
        psum = ctx.enter_context(tc.psum_pool(name="psum", bufs=1))

        def sbuf(shape, dtype, name, tag=None):
            return sb.tile(shape, dtype, name=name, tag=tag or name, align_bytes=256)

        banks = []

        def next_bank(number=None):
            if number is None:
                number = (banks[-1] + 1) % PSUM_BANKS if banks else 0
            banks.append(number)
            return psum.tile([P, BANK], F32, name="bank%d" % number)

        def list_half(tile, h):
            return tile[:, h * LIST_COLS // 2 : (h + 1) * LIST_COLS // 2]

        tab_list = lists.tile([P, LIST_COLS], U16, name="tab_list")
        slot_list = lists.tile([P, LIST_COLS], U16, name="slot_list")
        pair_list = lists.tile([P, LIST_COLS], U16, name="pair_list")
        tab_sc = sbuf([P, T], U8, "tab_sc")
        nc.vector.memset(tab_sc[32:64, :].bitcast(I32), 0)
        nc.vector.memset(tab_sc[64:, :].bitcast(I32), 0)
        v_sc = sbuf([P, S], U8, "v_sc")
        nc.gpsimd.memset(v_sc[:].bitcast(I32), 0)
        w4_sc = sbuf([P, N], U8, "w4_sc")
        nc.gpsimd.memset(w4_sc[:].bitcast(I32), 0)
        nc.sync.dma_start(tab_list[:], offs)
        news = [sbuf([P, S], F32, "new%d" % n) for n in range(PASSES * PACK)]

        def load_new(n, first, last, queue=nc.sync):
            g, i = divmod(n, PACK)
            xs_rows = xs[g * K_PASS : (g + 1) * K_PASS, :].rearrange("(p i) m -> p i m", i=PACK)[:, i, :]
            queue.dma_start(news[n][:, first:last], xs_rows[:, first:last])

        nc.scalar.dma_start(tab_sc[:32, :].bitcast(I32), tab_scales.rearrange("g q t -> (g q) t").bitcast(I32))
        picked_sc = sbuf([P, S], U8, "picked_sc")
        nc.vector.tensor_copy(picked_sc[:], tab_sc[:].indirect(tab_list[:]))

        planes = []

        def load_plane(n, first_new):
            g, i = divmod(n, PACK)
            plane = sbuf([P, T], F32, "plane%d" % n)
            if first_new:
                load_new(n, 0, first_new, nc.scalar)
                nc.sync.dma_start(slot_list[:], offs2)
            nc.sync.dma_start(plane[:], base[g * K_PASS : (g + 1) * K_PASS, :].rearrange("(p i) t -> p i t", i=PACK)[:, i, :])
            load_new(n, first_new, S)
            planes.append(plane)

        load_plane(0, FIRST_CUT)
        load_plane(1, 0)
        w1_raw = []
        for g in range(PASSES):
            raw = sbuf([P, PACK, H], F32, "w1_raw%d" % g)
            nc.sync.dma_start(raw[:], w1[g * K_PASS : (g + 1) * K_PASS, :].rearrange("(p i) r -> p i r", i=PACK))
            w1_raw.append(raw)
            load_plane(2 + g, 0)
        for n in range(4, 6):
            load_plane(n, 0)
        tab_hbm = [tab_words[g].rearrange("p t i -> p (t i)").bitcast(I32) for g in range(PASSES)]
        tab = []
        for g in range(PASSES):
            words = sbuf([P, T], I32, "tab%d" % g)
            nc.sync.dma_start(words[:], tab_hbm[g])
            tab.append(words)


        def move_scale_rows(g, q):
            src, dst = 16 * g + 4 * q, 32 * q + 4 * g
            nc.sync.dma_start(v_sc[dst : dst + 4, :].bitcast(I32), picked_sc[src : src + 4, :].bitcast(I32))

        load_plane(6, 0)
        for n in range(PASSES * QUADRANTS - 1):
            move_scale_rows(*divmod(n, QUADRANTS))
        load_plane(7, 0)
        move_scale_rows(PASSES - 1, QUADRANTS - 1)
        nc.sync.dma_start(pair_list[:], offs3)
        decay_sb = sbuf([P, PACK], F32, "decay_sb")
        gain_sb = sbuf([P, PACK], F32, "gain_sb")
        bias_sb = sbuf([P, N // P], F32, "bias_sb")
        w4 = sbuf([P, 2 * N], U8, "w4")
        nc.sync.dma_start(decay_sb[:], decay.rearrange("(p t) -> p t", t=PACK))
        nc.sync.dma_start(gain_sb[:], gain.rearrange("(p t) -> p t", t=PACK))
        with nc.allow_non_contiguous_dma(reason="one bias value a partition"):
            nc.sync.dma_start(bias_sb[:], bias.rearrange("(u p) -> p u", p=P))
        nc.sync.dma_start(w4[:].bitcast(I32), w4_words[0].bitcast(I32))
        for q in range(QUADRANTS):
            nc.sync.dma_start(
                w4_sc[32 * q : 32 * q + 4, :].bitcast(I32), w4_scales[0, 4 * q : 4 * q + 4, :].bitcast(I32)
            )

        def scatter(n):
            nc.vector.tensor_copy(planes[n][:].indirect(slot_list[:]), news[n][:])

        def chunk(c):
            return slice(c * BANK, (c + 1) * BANK)

        pairs = [sbuf([P, 2, PAGE_HALF, 2], BF16, "pairs%d" % h) for h in range(2)]

        def round_into_pairs(n):
            u, e = divmod(n % PACK, 2)
            for h in range(2):
                nc.scalar.copy(pairs[h][:, u, :, e], planes[n][:, h * PAGE_HALF : (h + 1) * PAGE_HALF])

        for first, last in ((0, FIRST_CUT), (FIRST_CUT, S)):
            nc.vector.tensor_copy(planes[0][:].indirect(slot_list[:, first // 16 : last // 16]), news[0][:, first:last])
        round_into_pairs(0)
        w1_woven = []
        for g in range(PASSES):
            woven = sbuf([P, PACK * H], BF16, "w1_bf%d" % g)
            nc.scalar.activation(
                woven[:].rearrange("p (t m i) -> p m i t", t=PACK, i=PACK),
                w1_raw[g][:].rearrange("p i (m t) -> p m i t", t=PACK),
                ACT.Copy,
            )
            w1_woven.append(woven)
        for n in range(1, PACK):
            scatter(n)
            round_into_pairs(n)
        woven0 = []
        for c in range(CHUNKS):
            h, part = divmod(c, 2)
            woven = sbuf([P, BANK * PACK], BF16, "woven0_%d" % c)
            nc.scalar.copy(
                woven[:].bitcast(F32).rearrange("p (c u) -> p c u", u=2),
                pairs[h][:, :, chunk(part), :].rearrange("p u c e -> p u (c e)").bitcast(F32).rearrange("p u c -> p c u"),
            )
            woven0.append(woven)

        woven1 = [sbuf([P, BANK, PACK], BF16, "woven1_%d" % c)[:] for c in range(2)]
        second_half = sbuf([P, PAGE_HALF, PACK], BF16, "woven1_half")
        woven1.extend(second_half[:, chunk(part), :] for part in range(2))
        for n in (4, 5):
            scatter(n)
            round_into_pairs(n)

        def words_of(c):
            return woven1[c].rearrange("p c i -> p (c i)").bitcast(F32).rearrange("p (c u) -> p c u", u=2)

        for c in (3, 0, 1):
            h, part = divmod(c, 2)
            nc.scalar.copy(words_of(c), pairs[h][:, 0, chunk(part), :].bitcast(F32).to_broadcast([P, BANK, 2]))

        def weave_on_scalar(n, c):
            nc.scalar.copy(woven1[c][:, :, n - PACK], planes[n][:, chunk(c)])

        def weave_on_gpsimd(n, c, one):
            nc.gpsimd.tensor_scalar(woven1[c][:, :, n - PACK], planes[n][:, chunk(c)], one, 0.0, ALU.mult, ALU.add)

        scatter(6)
        weave_on_gpsimd(6, 3, 1.0)
        for c in (0, 1):
            weave_on_scalar(6, c)
        nc.scalar.copy(pairs[1][:, 1, :BANK, 0], planes[6][:, chunk(2)])
        nc.scalar.copy(
            words_of(2),
            pairs[1][:, :, :BANK, :].rearrange("p u c e -> p u (c e)").bitcast(F32).rearrange("p u c -> p c u"),
        )
        scatter(7)
        for c in (0, 1):
            weave_on_scalar(7, c)
        nc.scalar.copy(woven1[2][:, :SHARED_CUT, 3], planes[7][:, 2 * BANK : 2 * BANK + SHARED_CUT])

        page1_codes, page1_sc = {}, {}
        held_sc = sbuf([P, 2, PAGE_HALF], U8, "held_sc", "new7")
        page0_codes = [sbuf([P, PAGE_HALF], U32, "page0_codes0")]
        page0_sc = [held_sc[:, h, :] for h in range(2)]

        def quantise_pass0(c):
            h, part = divmod(c, 2)
            nc.vector.quantize_mx(
                out=page0_codes[h][:, chunk(part)].bitcast(FP8X4), scales=page0_sc[h][:, chunk(part)], in_=woven0[c][:]
            )

        def quantise_pass1(c):
            codes = sbuf([P, BANK], U32, "page1_codes%d" % c)
            scales = sbuf([P, BANK], U8, "page1_sc%d" % c)
            nc.vector.quantize_mx(
                out=codes[:].bitcast(FP8X4), scales=scales[:], in_=woven1[c].rearrange("p c i -> p (c i)")
            )
            page1_codes[c], page1_sc[c] = codes, scales

        v_words = {}

        def gather_words(g, h, tag):
            words = sbuf([P, BANK], U32, "v%d_%d" % (g, h), tag)
            nc.vector.tensor_copy(words[:], tab[g][:].bitcast(U32).indirect(list_half(tab_list, h)))
            v_words[g, h] = words

        w1_codes = sbuf([P, PASSES * H], U32, "w1_codes", "new6")
        w1_sc = sbuf([P, PASSES * H], U8, "w1_sc", "picked_sc")

        def quantise_w1(g):
            cols = slice(g * H, (g + 1) * H)
            nc.vector.quantize_mx(out=w1_codes[:, cols].bitcast(FP8X4), scales=w1_sc[:, cols], in_=w1_woven[g][:])

        quantise_w1(0)
        quantise_pass0(0)
        quantise_w1(1)
        quantise_pass0(1)
        quantise_pass1(0)
        one = sbuf([P, 1], F32, "one", "woven1_0")
        nc.gpsimd.memset(one[:], 1.0)
        nc.gpsimd.tensor_tensor(
            second_half[:, 2 * P :, 3],
            planes[7][:, PAGE_HALF + 2 * P :],
            one[:].to_broadcast([P, PAGE_HALF - 2 * P]),
            ALU.mult,
        )
        gather_words(0, 0, "w1_bf1")
        gather_words(1, 0, "w1_bf0")
        gather_words(0, 1, "woven0_0")
        quantise_pass1(1)
        nc.vector.tensor_copy(woven1[2][:, P : 2 * P, 3], planes[7][:, 2 * BANK + P : 2 * BANK + 2 * P])
        page0_codes.append(sbuf([P, PAGE_HALF], U32, "page0_codes1", "woven1_0"))
        quantise_pass0(2)
        quantise_pass1(2)
        quantise_pass0(3)
        quantise_pass1(3)
        gather_words(1, 1, "woven0_3")

        def project(acc, t, moving, passes=range(PASSES)):
            for g in passes:
                cols = slice(g * H + t * P, g * H + (t + 1) * P)
                codes, scales = moving[g]
                nc.tensor.matmul_mx(
                    out=acc[:],
                    lhsT=w1_codes[:, cols].bitcast(FP8X4),
                    lhsT_scale=w1_sc[:, cols],
                    rhs=codes.bitcast(FP8X4),
                    rhs_scale=scales,
                    start=(g == 0),
                    stop=(g == PASSES - 1),
                )

        a_sb = [sbuf([P, T], F32, "a%d" % t, "plane%d" % t) for t in range(PACK)]

        def project_page(t, c, copy=nc.scalar.copy, bank=None):
            acc = next_bank(bank)
            h, part = divmod(c, 2)
            cols = slice(part * BANK, (part + 1) * BANK)
            project(acc, t, [(page0_codes[h][:, cols], page0_sc[h][:, cols]), (page1_codes[c][:], page1_sc[c][:])])
            copy(a_sb[t][:, chunk(c)], acc[:])

        diff = [sbuf([P, PACK, BANK], F32, "dist%d" % h, "pairs%d" % h) for h in range(2)]
        rate_parts = (
            (0, BANK, "page1_codes3"),
            (BANK, 2 * P, "woven1_0"),
            (S - 2 * P, P, "rate2"),
            (S - P, P, "rate3"),
        )
        rate = [sbuf([P, PACK, width], F32, "rate%d" % n, tag) for n, (j0, width, tag) in enumerate(rate_parts)]

        def table_operands(h):
            return [(v_words[g, h][:], v_sc[4 * g :, chunk(h)]) for g in range(PASSES)]

        def fetch_b(t, h, tag, bank=None):
            acc = next_bank(bank)
            project(acc, t, table_operands(h))
            b_sb = sbuf([P, BANK], F32, "b%d_%d" % (t, h), tag)
            nc.scalar.copy(b_sb[:], acc[:])
            return b_sb

        def gather_minus_b(t, h, b_sb):
            nc.vector.tensor_tensor(diff[h][:, t, :], a_sb[t][:].indirect(list_half(pair_list, h)), b_sb[:], ALU.subtract)

        def scale_distances(part):
            j0, width, tag = rate_parts[part]
            h, c0 = divmod(j0, BANK)
            for t in range(PACK):
                nc.scalar.activation(
                    rate[part][:, t, :], diff[h][:, t, c0 : c0 + width], ACT.Abs, scale=decay_sb[:, t : t + 1]
                )

        def similarity(n, part, c0, width, tag):
            sim = sbuf([P, PACK, width], F32, "sim%d" % n, tag)
            nc.scalar.activation(sim[:], rate[part][:, :, c0 : c0 + width], ACT.Exp, scale=-1.0)
            return sim

        def weigh(z, sim):
            width = z.shape[1]
            nc.vector.tensor_tensor(
                z.rearrange("p (c e) t -> p c t e", e=2),
                sim[:].rearrange("p t (c e) -> p c t e", e=2),
                gain_sb[:].unsqueeze(1).unsqueeze(3).to_broadcast([P, width // 2, PACK, 2]),
                ALU.mult,
            )

        def product_with_w4(n, z, width, codes_tag):
            codes = sbuf([P, width], U32, "z_codes%d" % n, codes_tag)
            scales = sbuf([P, width], U8, "z_sc%d" % n)
            nc.vector.quantize_mx(out=codes[:].bitcast(FP8X4), scales=scales[:], in_=z.rearrange("p c t -> p (c t)"))

            def rows(u, acc=None):
                if acc is None:
                    acc = next_bank()[:, :width]
                nc.tensor.matmul_mx(
                    out=acc,
                    lhsT=w4[:, 2 * P * u : 2 * P * (u + 1)].bitcast(FP4X4),
                    lhsT_scale=w4_sc[:, P * u : P * (u + 1)],
                    rhs=codes[:].bitcast(FP8X4),
                    rhs_scale=scales[:],
                    start=True,
                    stop=True,
                )
                return acc

            return rows

        def store_by_scalar(acc, res, u, j0, queue):
            nc.scalar.activation(res[:], acc, ACT.Identity, bias=bias_sb[:, u : u + 1])
            queue.dma_start(out[u * P : (u + 1) * P, j0 : j0 + res.shape[1]], res[:])

        b_sb = {}
        for t in range(PACK):
            project_page(t, 0)
        first_b = [next_bank() for t in range(PACK)]
        for step in range(PACK + 1):
            for g in range(PASSES):
                if 0 <= step - g < PACK:
                    project(first_b[step - g], step - g, table_operands(0), (g,))
        for t in range(PACK):
            b_sb[t, 0] = sbuf([P, BANK], F32, "b%d_0" % t, "new%d" % (2 + t))
            nc.scalar.copy(b_sb[t, 0][:], first_b[t][:])
        for t in range(PACK - 1):
            project_page(t, 1)
        project_page(0, 2, bank=3)
        project_page(2, 2)
        project_page(0, 3)
        project_page(1, 2, copy=nc.vector.tensor_copy)
        project_page(1, 3)
        project_page(2, 3)
        project_page(3, 1, bank=3)
        project_page(3, 2, bank=1)
        project_page(3, 3)
        for t in range(PACK):
            b_sb[t, 1] = fetch_b(t, 1, ("b0", "plane4", "plane5", "plane6")[t], 4 + t)
        for h in range(2):
            for t in range(PACK):
                gather_minus_b(t, h, b_sb[t, h])

        quarter = BANK // 2
        scale_distances(0)
        sim0 = [similarity(0, 0, 0, quarter, "w1_raw0"), similarity(1, 0, quarter, quarter, "w1_raw1")]
        scale_distances(1)
        sim1 = similarity(2, 1, 0, quarter, "woven0_0")
        scale_distances(2)
        scale_distances(3)
        sim2 = similarity(3, 2, 0, P, "new0")
        sim3 = similarity(4, 3, 0, P, "plane7")
        z0 = sbuf([P, BANK, PACK], BF16, "z0", "plane2")
        for q in range(2):
            weigh(z0[:, q * quarter : (q + 1) * quarter, :], sim0[q])
        votes0 = [product_with_w4(0, z0[:, :quarter, :], quarter, "z_codes0")]
        z1 = sbuf([P, quarter, PACK], BF16, "z1", "b0")
        weigh(z1[:], sim1)
        votes0.append(product_with_w4(4, z0[:, quarter:, :], quarter, "z_codes4"))
        z2 = sbuf([P, P, PACK], BF16, "z2", "new1")
        weigh(z2[:], sim2)
        votes1 = product_with_w4(1, z1[:], quarter, rate_parts[2][2])
        z3 = sbuf([P, P, PACK], BF16, "z3")
        weigh(z3[:], sim3)
        votes2 = product_with_w4(2, z2[:], P, rate_parts[3][2])
        votes3 = product_with_w4(3, z3[:], P, "z_codes3")
        for u in range(N // P):
            acc = next_bank()
            for q in range(2):
                votes0[q](u, acc[:, q * quarter : (q + 1) * quarter])
            store_by_scalar(acc[:], sbuf([P, BANK], F32, "res0_%d" % u, ("woven0_0", "new0")[u]), u, 0, nc.sync)
        store_by_scalar(votes1(0), sbuf([P, quarter], F32, "res1_0"), 0, BANK, nc.sync)
        res = sbuf([P, quarter], F32, "res1_1", "z3")
        nc.vector.tensor_scalar(res[:], votes1(1), bias_sb[:, 1:2], None, ALU.add)
        nc.sync.dma_start(out[P : 2 * P, BANK : BANK + quarter], res[:])
        j_last = BANK + quarter
        last = [next_bank(), next_bank()]
        for votes, c0 in ((votes2, 0), (votes3, P)):
            for u in range(N // P):
                votes(u, last[u][:, c0 : c0 + P])
        store_by_scalar(last[0][:, :quarter], sbuf([P, quarter], F32, "res2_0", "tab0"), 0, j_last, nc.scalar)
        res = sbuf([P, quarter], F32, "res2_1", "tab1")
        nc.vector.tensor_scalar(res[:], last[1][:, :quarter], bias_sb[:, 1:2], None, ALU.add)
        nc.sync.dma_start(out[P : 2 * P, j_last : j_last + quarter], res[:])
